import numpy as np
import ml_dtypes


def mxq(x, axis, fmt="e4m3"):
    dtype, down = {"e4m3": (ml_dtypes.float8_e4m3fn, 7), "e5m2": (ml_dtypes.float8_e5m2, 14)}[fmt]
    v = np.moveaxis(np.asarray(x, np.float32).astype(ml_dtypes.bfloat16).astype(np.float64), axis, -1)
    blocks = v.reshape(v.shape[:-1] + (-1, 32))
    amax = np.abs(blocks).max(-1, keepdims=True)
    byte = np.maximum(np.where(amax > 0, np.frexp(amax)[1] - 1 + 127, 0) - down, 1)
    scale = np.exp2(byte - 127.0)
    codes = (blocks / scale).astype(np.float32).astype(dtype).astype(np.float64)
    return np.moveaxis((codes * scale).reshape(v.shape), -1, axis)


WIDE = False


def mx_kscale(k):
    if not WIDE:
        return np.ones(k)
    levels = np.array([10, -10, 5, -5, 0])
    if k % 512:
        return np.exp2(np.random.permutation(np.resize(levels, k // 32))).repeat(32)
    a = np.empty((k // 512, 16))
    for p in range(k // 512):
        a[p, :8] = np.random.permutation(np.resize(levels, 8))
        for g in range(8):
            far = levels[np.abs(levels - a[p, g]) >= 10]
            a[p, g + 8] = far[np.random.randint(len(far))]
    return np.exp2(a.ravel()).repeat(32)


def f64(x):
    return np.asarray(x).astype(np.float64)


def striped(idx):
    return np.tile(idx.reshape(-1, 16).T, (8, 1)).astype(np.uint16)


def unstriped(offs):
    return offs[:16].T.reshape(-1).astype(np.int64)


E2M1 = np.array([0.0, 0.5, 1.0, 1.5, 2.0, 3.0, 4.0, 6.0, -0.0, -0.5, -1.0, -1.5, -2.0, -3.0, -4.0, -6.0])


def pack_weight(w, fmt):
    k, n = w.shape
    w = f64(np.asarray(w, np.float32).astype(ml_dtypes.bfloat16)).reshape(k // 32, 32, n)
    amax = np.abs(w).max(1)
    if fmt == "e4m3":
        byte = np.frexp(amax)[1] - 1 + 127 - 7
    else:
        mant, ex = np.frexp(amax / 6.0)
        byte = np.where(mant > 0.5, ex, ex - 1) + 127
    byte = np.clip(np.where(amax > 0, byte, 1), 1, 254)
    scaled = (w * np.exp2(127.0 - byte)[:, None, :]).reshape(k, n).astype(np.float32)
    by_word = np.ascontiguousarray(scaled.reshape(k // 512, 128, 4, n).transpose(0, 1, 3, 2))
    if fmt == "e4m3":
        words = by_word.astype(ml_dtypes.float8_e4m3fn).view(np.uint8)
    else:
        c = by_word.astype(ml_dtypes.float4_e2m1fn).view(np.uint8) & 0xF
        words = (c[..., 0::2] | (c[..., 1::2] << 4)).reshape(k // 512, 128, 2 * n)
    return np.ascontiguousarray(words), np.ascontiguousarray(byte.astype(np.uint8).reshape(k // 512, 16, n))


def unpack_weight(words, scales, fmt):
    g, _, n = scales.shape
    words = np.ascontiguousarray(words).reshape(g, 128, n, -1)
    if fmt == "e4m3":
        vals = words.view(ml_dtypes.float8_e4m3fn).astype(np.float64)
    else:
        nib = np.empty((g, 128, n, 4), np.uint8)
        nib[..., 0::2] = words & 0xF
        nib[..., 1::2] = words >> 4
        vals = E2M1[nib]
    vals = vals * np.repeat(np.exp2(scales.astype(np.float64) - 127.0), 8, axis=1)[..., None]
    return vals.transpose(0, 1, 3, 2).reshape(g * 512, n)


def gelu(v):
    return 0.5 * v * (1.0 + np.tanh(np.sqrt(2.0 / np.pi) * (v + 0.044715 * v**3)))


K, T, S, P, H, N = 1536, 4096, 1024, 512, 1024, 384


def setup_inputs():
    n = np.random.standard_normal
    s = mx_kscale(K)[:, None]
    u = mx_kscale(H)[:, None]
    tab_words, tab_scales = pack_weight(n((K, T)) * s, "e4m3")
    w4_words, w4_scales = pack_weight(n((K, H)) / np.sqrt(K) / s, "e2m1")
    return {
        "tab_words": tab_words,
        "tab_scales": tab_scales,
        "offs": striped(np.random.permutation(T)[:S]),
        "w4_words": w4_words,
        "w4_scales": w4_scales,
        "pos1": striped(np.random.permutation(S)[:P]),
        "pos2": striped(np.random.permutation(S)[:P]),
        "pos3": striped(np.random.permutation(S)[:P]),
        "gain": (np.exp(0.3 * n(H)) * u[:, 0]).astype(np.float32),
        "w2": (n((H, N)) / np.sqrt(H) / u).astype(np.float32),
    }


def reference(tab_words, tab_scales, offs, w4_words, w4_scales, pos1, pos2, pos3, gain, w2):
    v = unpack_weight(tab_words, tab_scales, "e4m3")[:, unstriped(offs)]
    w4 = unpack_weight(w4_words, w4_scales, "e2m1")
    h = w4.T @ v
    o = h[:, unstriped(pos1)]
    t = h[:, unstriped(pos2)]
    d = h[:, unstriped(pos3)]
    z = f64(gain)[:, None] * (1.0 / (1.0 + np.exp(-o)) * (1.0 + t * (1.0 + d)))
    return mxq(f64(w2), 0, "e4m3").T @ mxq(z, 0, "e4m3")

@@ -1,0 +1,267 @@
+from contextlib import ExitStack
+
+import concourse.mybir as mybir
+
+K, T, S, LINES, H, N = 1536, 4096, 1024, 512, 1024, 384
+FLOPS = 2 * K * H * S + 2 * H * N * LINES
+
+F32 = mybir.dt.float32
+BF16 = mybir.dt.bfloat16
+I32 = mybir.dt.int32
+U32 = mybir.dt.uint32
+U16 = mybir.dt.uint16
+U8 = mybir.dt.uint8
+FP8X4 = mybir.dt.float8_e4m3fn_x4
+FP4X4 = mybir.dt.float4_e2m1fn_x4
+ACT = mybir.ActivationFunctionType
+MULT, ADD = mybir.AluOpType.mult, mybir.AluOpType.add
+
+P = 128
+PACK = 4
+K_PASS = P * PACK
+PASSES = K // K_PASS
+GROUPS = H // K_PASS
+BANK = 512
+WINDOW = 2048
+HALF = LINES // 2
+H_TILES = 4
+SLOTS = GROUPS * PACK
+
+
+def tile_list_corridor_boardings_kernel(
+    tc, tab_words, tab_scales, offs, w4_words, w4_scales, pos1, pos2, pos3, gain, w2, out
+):
+    nc = tc.nc
+    with ExitStack() as ctx:
+        keep = ctx.enter_context(tc.tile_pool(name="keep", bufs=1))
+        ring = ctx.enter_context(tc.tile_pool(name="ring", bufs=2))
+        psum = ctx.enter_context(tc.psum_pool(name="psum", bufs=8))
+
+        stops = keep.tile([P, S // 16], U16, name="stops")
+        nc.sync.dma_start(stops[:], offs)
+
+        table = [keep.tile([P, T], I32, name=f"table{a}", tag=f"table{a}", align_bytes=64) for a in range(PASSES)]
+        w4_raw = keep.tile([P, PASSES, H // 2], I32, name="w4_raw", tag="w4_raw", align_bytes=64)
+
+        def load_table(a):
+            nc.sync.dma_start(table[a][:], tab_words[a].rearrange("p t i -> p (t i)").bitcast(I32))
+
+        load_table(0)
+        nc.sync.dma_start(w4_raw[:], w4_words.bitcast(I32).rearrange("a p w -> p a w"))
+        load_table(1)
+        load_table(2)
+
+        scale_window = keep.tile([P, T], U8, name="scale_window", tag="scale_window", align_bytes=64)
+        nc.gpsimd.memset(scale_window[:].bitcast(I32), 0)
+        for q in range(4):
+            nc.gpsimd.dma_start(
+                scale_window[32 * q : 32 * q + 4 * PASSES, :].bitcast(I32),
+                tab_scales[:, 4 * q : 4 * q + 4, :].bitcast(I32),
+            )
+        w4s_raw = keep.tile([P, PASSES, H // 4], I32, name="w4s_raw", tag="w4s_raw", align_bytes=64)
+        for q in range(4):
+            nc.scalar.dma_start(
+                w4s_raw[32 * q : 32 * q + 4],
+                w4_scales[:, 4 * q : 4 * q + 4, :].bitcast(I32).rearrange("a r w -> r a w"),
+            )
+
+        lists = []
+        for name, src in (("origin", pos1), ("transfer", pos2), ("dest", pos3)):
+            tile = keep.tile([P, LINES // 16], U16, name=name)
+            nc.sync.dma_start(tile[:], src)
+            lists.append(tile)
+        origin, transfer, dest = lists
+
+        gain_by_slot = gain.rearrange("(b g t i) -> b t g i", b=GROUPS, t=PACK, i=8)
+        gains = []
+        with nc.allow_non_contiguous_dma(reason="one gain to a partition"):
+            for j in range(SLOTS):
+                tile = keep.tile([P, 1], F32, name=f"gain{j}")
+                nc.sync.dma_start(tile[:], gain_by_slot[j // PACK, j % PACK].unsqueeze(2))
+                gains.append(tile[:])
+        w2_by_slot = w2.rearrange("(b g t i) n -> b t g i n", b=GROUPS, t=PACK, i=8)
+        late = keep.tile([P, SLOTS * N], F32, name="late")
+        for j in range(SLOTS):
+            nc.sync.dma_start(late[:, N * j : N * (j + 1)], w2_by_slot[j // PACK, j % PACK])
+
+        warm = keep.tile([P, 1], F32, name="warm")
+        nc.vector.memset(warm[:], 0.0)
+        warm_out = keep.tile([P, 1], F32, name="warm_out")
+        nc.scalar.activation(warm_out[:], warm[:], ACT.Sigmoid)
+
+        h_tiles = [keep.tile([P, WINDOW], F32, name=f"h{x}") for x in range(H_TILES)]
+        w4s = keep.tile([P, PASSES, H], U8, name="w4s", align_bytes=64)
+        nc.vector.memset(w4s[:].bitcast(I32), 0)
+        for q in range(4):
+            rows = slice(32 * q, 32 * q + 4)
+            nc.vector.tensor_copy(
+                w4s[rows].bitcast(I32).rearrange("p a (b t g w) -> p (a b) t g w", b=GROUPS, t=PACK, w=2),
+                w4s_raw[rows].rearrange("p a (b g t w) -> p (a b) t g w", b=GROUPS, t=PACK, w=2),
+            )
+        planes = [keep.tile([P, S], U8, name="plane0", tag="w4s_raw", align_bytes=64)]
+        for a in range(1, PASSES):
+            planes.append(keep.tile([P, S], U8, name=f"plane{a}", align_bytes=64))
+            nc.vector.memset(planes[a][96:P, :].bitcast(I32), 0)
+        nc.vector.tensor_copy(planes[0][:], scale_window[:].indirect(stops[:]))
+        for a in range(1, PASSES):
+            nc.gpsimd.dma_start(planes[a][0:112, :].bitcast(I32), planes[0][4 * a : 4 * a + 112, :].bitcast(I32))
+
+        w4 = keep.tile([P, PASSES, 2 * H], U8, name="w4", align_bytes=64)
+        picked = {}
+
+        def gather(a, width, tag):
+            picked[a] = keep.tile([P, S], U32, name=f"picked{a}", tag=tag, align_bytes=64)
+            for lo in range(0, S, width):
+                offsets = stops[:, lo // 16 : (lo + width) // 16]
+                nc.vector.tensor_copy(picked[a][:, lo : lo + width], table[a][:].bitcast(U32).indirect(offsets))
+
+        gather(0, S, "scale_window")
+        nc.vector.tensor_copy(
+            w4[:].bitcast(I32).rearrange("p a (b t g w) -> p (a b) t g w", b=GROUPS, t=PACK, w=4),
+            w4_raw[:].rearrange("p a (b g t w) -> p (a b) t g w", b=GROUPS, t=PACK, w=4),
+        )
+        gather(1, S, "table0")
+        gather(2, BANK, "table1")
+
+        banks = {}
+
+        def first_product(j, c, a):
+            if a == 0:
+                banks[j, c] = psum.tile([P, BANK], F32, name="bank", tag="bank")
+            nc.tensor.matmul_mx(
+                banks[j, c][:],
+                lhsT=w4[:, a, 2 * P * j : 2 * P * (j + 1)].bitcast(FP4X4),
+                lhsT_scale=w4s[:, a, P * j : P * (j + 1)],
+                rhs=picked[a][:, BANK * c : BANK * (c + 1)].bitcast(FP8X4),
+                rhs_scale=planes[a][:, BANK * c : BANK * (c + 1)],
+                start=(a == 0),
+                stop=(a == PASSES - 1),
+            )
+
+        EARLY = 4
+        for a in range(PASSES - 1):
+            for j in range(EARLY):
+                for c in range(2):
+                    first_product(j, c, a)
+
+        w2_codes = keep.tile([P, GROUPS, N], U32, name="w2_codes", align_bytes=64)
+        w2_scales = keep.tile([P, GROUPS, N], U8, name="w2_scales", align_bytes=64)
+        w2_woven = keep.tile([P, GROUPS, N, PACK], BF16, name="w2_woven", align_bytes=64)
+
+        def weave_w2(b):
+            nc.scalar.copy(
+                w2_woven[:, b].rearrange("p (c i) t -> p c t i", i=4),
+                late[:, PACK * N * b : PACK * N * (b + 1)].rearrange("p (t c i) -> p c t i", t=PACK, i=4),
+            )
+
+        def quantize_w2():
+            flat = w2_woven[:].rearrange("p b n t -> p (b n t)")
+            codes = w2_codes[:].rearrange("p b n -> p (b n)")
+            scales = w2_scales[:].rearrange("p b n -> p (b n)")
+            for lo, hi in ((0, 512), (512, 768)):
+                nc.vector.quantize_mx(codes[:, lo:hi].bitcast(FP8X4), scales[:, lo:hi], flat[:, PACK * lo : PACK * hi])
+
+        gate = [keep.tile([P, PACK, LINES], F32, name=f"gate{b}") for b in range(GROUPS)]
+        poly = [keep.tile([P, PACK, LINES], F32, name=f"poly{b}") for b in range(GROUPS)]
+        inner = {}
+
+        def features(j):
+            for c in range(2):
+                for a in range(PASSES - 1 if j < EARLY else 0, PASSES):
+                    first_product(j, c, a)
+            h = h_tiles[j % H_TILES]
+            nc.scalar.copy(h[:, 0:BANK], banks[j, 0][:])
+            if j == 0:
+                nc.vector.tensor_copy(h[:, BANK:S], banks[j, 1][:])
+            else:
+                nc.scalar.copy(h[:, BANK:S], banks[j, 1][:])
+
+        def pieces(j):
+            return ((0, HALF), (HALF, LINES)) if j == SLOTS - 1 else ((0, LINES),)
+
+        def look_up(j):
+            h = h_tiles[j % H_TILES]
+            one_d = ring.tile([P, LINES], F32, name="one_d")
+            nc.vector.tensor_scalar(one_d[:], h[:].indirect(dest[:]), 1.0, 1.0, MULT, ADD)
+            nc.scalar.activation(gate[j // PACK][:, j % PACK, :], h[:].indirect(origin[:]), ACT.Sigmoid)
+            inner[j] = ring.tile([P, LINES], F32, name="inner", bufs=3)
+            for lo, hi in pieces(j):
+                offsets = transfer[:, lo // 16 : hi // 16]
+                nc.vector.tensor_tensor(inner[j][:, lo:hi], h[:].indirect(offsets), one_d[:, lo:hi], MULT)
+
+        def add_gain(j):
+            for lo, hi in pieces(j):
+                nc.scalar.activation(
+                    poly[j // PACK][:, j % PACK, lo:hi], inner[j][:, lo:hi], ACT.Identity, bias=gains[j], scale=gains[j]
+                )
+
+        z_codes = keep.tile([P, GROUPS, LINES], U32, name="z_codes", align_bytes=64)
+        z_scales = keep.tile([P, GROUPS, LINES], U8, name="z_scales", align_bytes=64)
+        woven = keep.tile([P, GROUPS, LINES, PACK], BF16, name="woven", align_bytes=64)
+
+        def weave_z(b, cols):
+            nc.vector.tensor_tensor(
+                woven[:, b, cols].rearrange("p (c i) t -> p c t i", i=4),
+                poly[b][:, :, cols].rearrange("p t (c i) -> p c t i", i=4),
+                gate[b][:, :, cols].rearrange("p t (c i) -> p c t i", i=4),
+                MULT,
+            )
+
+        def quantize_z(b, cols):
+            nc.vector.quantize_mx(
+                z_codes[:, b, cols].bitcast(FP8X4), z_scales[:, b, cols], woven[:, b, cols].rearrange("p m t -> p (m t)")
+            )
+
+        features(0)
+        for j in range(SLOTS):
+            look_up(j)
+            if j + 1 < SLOTS:
+                features(j + 1)
+            if j > 0:
+                add_gain(j - 1)
+            if j == PACK:
+                weave_z(0, slice(0, LINES))
+            if j in (2, 4):
+                weave_w2(j // 2 - 1)
+            if j == 4:
+                quantize_w2()
+                quantize_z(0, slice(0, LINES))
+        add_gain(SLOTS - 1)
+
+        def second_product(target, n, b, cols):
+            nc.tensor.matmul_mx(
+                target,
+                lhsT=w2_codes[:, b, P * n : P * (n + 1)].bitcast(FP8X4),
+                lhsT_scale=w2_scales[:, b, P * n : P * (n + 1)],
+                rhs=z_codes[:, b, cols].bitcast(FP8X4),
+                rhs_scale=z_scales[:, b, cols],
+                start=(b == 0),
+                stop=(b == GROUPS - 1),
+            )
+
+        classes = N // P
+        runs = [slice(lo, lo + P) for lo in range(0, LINES, P)]
+        out_by_class = out.rearrange("(n p) m -> p n m", p=P)
+        last_sums = [psum.tile([P, BANK], F32, name="bank", tag="bank") for n in range(classes)]
+        for n in range(classes):
+            second_product(last_sums[n][:, 0:P], n, 0, runs[-1])
+        weave_z(1, runs[0])
+        for u, cols in enumerate(runs):
+            result = keep.tile([P, classes, P], F32, name=f"result{u}")
+            if u + 1 < len(runs):
+                weave_z(1, runs[u + 1])
+                quantize_z(1, cols)
+                sums = psum.tile([P, BANK], F32, name="bank", tag="bank")
+                for n in range(classes):
+                    for b in range(GROUPS):
+                        second_product(sums[:, P * n : P * (n + 1)], n, b, cols)
+                nc.scalar.copy(result[:].rearrange("p n m -> p (n m)"), sums[:, 0 : classes * P])
+            else:
+                quantize_z(1, cols)
+                for n in range(classes):
+                    second_product(last_sums[n][:, 0:P], n, 1, cols)
+                    if n == 1:
+                        nc.vector.tensor_copy(result[:, n, :], last_sums[n][:, 0:P])
+                    else:
+                        nc.scalar.copy(result[:, n, :], last_sums[n][:, 0:P])
+            nc.sync.dma_start(out_by_class[:, :, cols], result[:])

@@ -24,8 +24,10 @@ GROUPS = H // K_PASS
 BANK = 512
 WINDOW = 2048
 HALF = LINES // 2
-H_TILES = 4
+H_TILES = 6
 SLOTS = GROUPS * PACK
+AHEAD = 2
+GAIN_ON_VECTOR = (0, 1, 2)
 
 
 def tile_list_corridor_boardings_kernel(
@@ -35,35 +37,19 @@ def tile_list_corridor_boardings_kernel(
     with ExitStack() as ctx:
         keep = ctx.enter_context(tc.tile_pool(name="keep", bufs=1))
         ring = ctx.enter_context(tc.tile_pool(name="ring", bufs=2))
+        shared = ctx.enter_context(tc.tile_pool(name="shared", bufs=1))
         psum = ctx.enter_context(tc.psum_pool(name="psum", bufs=8))
 
         stops = keep.tile([P, S // 16], U16, name="stops")
         nc.sync.dma_start(stops[:], offs)
 
-        table = [keep.tile([P, T], I32, name=f"table{a}", tag=f"table{a}", align_bytes=64) for a in range(PASSES)]
-        w4_raw = keep.tile([P, PASSES, H // 2], I32, name="w4_raw", tag="w4_raw", align_bytes=64)
-
-        def load_table(a):
-            nc.sync.dma_start(table[a][:], tab_words[a].rearrange("p t i -> p (t i)").bitcast(I32))
-
-        load_table(0)
-        nc.sync.dma_start(w4_raw[:], w4_words.bitcast(I32).rearrange("a p w -> p a w"))
-        load_table(1)
-        load_table(2)
-
-        scale_window = keep.tile([P, T], U8, name="scale_window", tag="scale_window", align_bytes=64)
-        nc.gpsimd.memset(scale_window[:].bitcast(I32), 0)
-        for q in range(4):
-            nc.gpsimd.dma_start(
-                scale_window[32 * q : 32 * q + 4 * PASSES, :].bitcast(I32),
-                tab_scales[:, 4 * q : 4 * q + 4, :].bitcast(I32),
-            )
-        w4s_raw = keep.tile([P, PASSES, H // 4], I32, name="w4s_raw", tag="w4s_raw", align_bytes=64)
-        for q in range(4):
-            nc.scalar.dma_start(
-                w4s_raw[32 * q : 32 * q + 4],
-                w4_scales[:, 4 * q : 4 * q + 4, :].bitcast(I32).rearrange("a r w -> r a w"),
-            )
+        scale_window = keep.tile([P, T], U8, name="scale_window", tag="scale_window")
+        scale_rows = tab_scales.bitcast(I32).rearrange("a q w -> (a q) w")
+        row_base = (96, 112, 16)
+        nc.sync.dma_start(scale_window[96:P, :].bitcast(I32), scale_rows[0:32])
+        nc.sync.dma_start(scale_window[16:32, :].bitcast(I32), scale_rows[32:48])
+        for lo, hi in ((0, 16), (32, 64), (64, 96)):
+            nc.vector.memset(scale_window[lo:hi, :].bitcast(I32), 0)
 
         lists = []
         for name, src in (("origin", pos1), ("transfer", pos2), ("dest", pos3)):
@@ -72,17 +58,34 @@ def tile_list_corridor_boardings_kernel(
             lists.append(tile)
         origin, transfer, dest = lists
 
-        gain_by_slot = gain.rearrange("(b g t i) -> b t g i", b=GROUPS, t=PACK, i=8)
-        gains = []
-        with nc.allow_non_contiguous_dma(reason="one gain to a partition"):
-            for j in range(SLOTS):
-                tile = keep.tile([P, 1], F32, name=f"gain{j}")
-                nc.sync.dma_start(tile[:], gain_by_slot[j // PACK, j % PACK].unsqueeze(2))
-                gains.append(tile[:])
-        w2_by_slot = w2.rearrange("(b g t i) n -> b t g i n", b=GROUPS, t=PACK, i=8)
-        late = keep.tile([P, SLOTS * N], F32, name="late")
-        for j in range(SLOTS):
-            nc.sync.dma_start(late[:, N * j : N * (j + 1)], w2_by_slot[j // PACK, j % PACK])
+        table = {}
+
+        def load_table(a, tile):
+            table[a] = tile
+            nc.sync.dma_start(tile[:], tab_words[a].rearrange("p t i -> p (t i)").bitcast(I32))
+
+        w4_by_group = w4_words.bitcast(I32).rearrange("a p (b w) -> b p a w", b=GROUPS)
+        w4 = [keep.tile([P, PASSES, 2 * K_PASS], U8, name=f"w4_{b}", align_bytes=64) for b in range(GROUPS)]
+
+        def order_w4(b, raw):
+            nc.vector.tensor_copy(
+                w4[b][:].bitcast(I32).rearrange("p a (t g w) -> p a t g w", t=PACK, w=4),
+                raw.rearrange("p (a g t w) -> p a t g w", a=PASSES, t=PACK, w=4),
+            )
+
+        W4_WORDS = PASSES * K_PASS // 2
+        w4_raw = keep.tile([P, W4_WORDS], I32, name="w4_raw")
+        nc.sync.dma_start(w4_raw[:].rearrange("p (a w) -> p a w", a=PASSES), w4_by_group[0])
+        load_table(0, keep.tile([P, T], I32, name="table0", tag="table0", align_bytes=64))
+        load_table(1, shared.tile([P, T], I32, name="table1", offset=0))
+
+        w4s_raw = keep.tile([P, PASSES, H // 4], I32, name="w4s_raw")
+        nc.gpsimd.memset(w4s_raw[:], 0)
+        for q in range(4):
+            nc.gpsimd.dma_start(
+                w4s_raw[32 * q : 32 * q + 4],
+                w4_scales[:, 4 * q : 4 * q + 4, :].bitcast(I32).rearrange("a r w -> r a w"),
+            )
 
         warm = keep.tile([P, 1], F32, name="warm")
         nc.vector.memset(warm[:], 0.0)
@@ -90,38 +93,50 @@ def tile_list_corridor_boardings_kernel(
         nc.scalar.activation(warm_out[:], warm[:], ACT.Sigmoid)
 
         h_tiles = [keep.tile([P, WINDOW], F32, name=f"h{x}") for x in range(H_TILES)]
-        w4s = keep.tile([P, PASSES, H], U8, name="w4s", align_bytes=64)
-        nc.vector.memset(w4s[:].bitcast(I32), 0)
-        for q in range(4):
-            rows = slice(32 * q, 32 * q + 4)
-            nc.vector.tensor_copy(
-                w4s[rows].bitcast(I32).rearrange("p a (b t g w) -> p (a b) t g w", b=GROUPS, t=PACK, w=2),
-                w4s_raw[rows].rearrange("p a (b g t w) -> p (a b) t g w", b=GROUPS, t=PACK, w=2),
-            )
-        planes = [keep.tile([P, S], U8, name="plane0", tag="w4s_raw", align_bytes=64)]
-        for a in range(1, PASSES):
-            planes.append(keep.tile([P, S], U8, name=f"plane{a}", align_bytes=64))
-            nc.vector.memset(planes[a][96:P, :].bitcast(I32), 0)
-        nc.vector.tensor_copy(planes[0][:], scale_window[:].indirect(stops[:]))
-        for a in range(1, PASSES):
-            nc.gpsimd.dma_start(planes[a][0:112, :].bitcast(I32), planes[0][4 * a : 4 * a + 112, :].bitcast(I32))
+        picked_scales = keep.tile([P, S], U8, name="picked_scales")
+        nc.vector.tensor_copy(picked_scales[:], scale_window[:].indirect(stops[:]))
+        planes = [keep.tile([P, S], U8, name=f"plane{a}", align_bytes=64) for a in range(PASSES)]
+        for a in range(PASSES):
+            nc.vector.memset(planes[a][:].bitcast(I32), 0)
 
-        w4 = keep.tile([P, PASSES, 2 * H], U8, name="w4", align_bytes=64)
+        for x in range(4 * PASSES):
+            a, q = divmod(x, 4)
+            first = row_base[a] + 4 * q
+            nc.sync.dma_start(planes[a][32 * q : 32 * q + 4, :].bitcast(I32), picked_scales[first : first + 4, :].bitcast(I32))
+            if x == 5:
+                load_table(2, keep.tile([P, T], I32, name="table2", tag="scale_window"))
+        order_w4(0, w4_raw[:])
+
         picked = {}
 
-        def gather(a, width, tag):
-            picked[a] = keep.tile([P, S], U32, name=f"picked{a}", tag=tag, align_bytes=64)
+        def gather(a, width, tile):
+            picked[a] = tile
             for lo in range(0, S, width):
                 offsets = stops[:, lo // 16 : (lo + width) // 16]
                 nc.vector.tensor_copy(picked[a][:, lo : lo + width], table[a][:].bitcast(U32).indirect(offsets))
 
-        gather(0, S, "scale_window")
+        gather(0, S, keep.tile([P, S], U32, name="picked0", align_bytes=64))
+
+        w4s = keep.tile([P, PASSES, H], U8, name="w4s", tag="table0", align_bytes=64)
         nc.vector.tensor_copy(
-            w4[:].bitcast(I32).rearrange("p a (b t g w) -> p (a b) t g w", b=GROUPS, t=PACK, w=4),
-            w4_raw[:].rearrange("p a (b g t w) -> p (a b) t g w", b=GROUPS, t=PACK, w=4),
+            w4s[:].bitcast(I32).rearrange("p a (b t g w) -> p (a b) t g w", b=GROUPS, t=PACK, w=2),
+            w4s_raw[:].rearrange("p a (b g t w) -> p (a b) t g w", b=GROUPS, t=PACK, w=2),
         )
-        gather(1, S, "table0")
-        gather(2, BANK, "table1")
+        gather(1, BANK, keep.tile([P, S], U32, name="picked1", align_bytes=64))
+        late = shared.tile([P, SLOTS * (N + 8)], F32, name="late", offset=0)
+        w4_late = shared.tile([P, W4_WORDS], I32, name="w4_late", offset=4 * SLOTS * (N + 8))
+        nc.sync.dma_start(w4_late[:].rearrange("p (a w) -> p a w", a=PASSES), w4_by_group[1])
+        gain_by_slot = gain.rearrange("(b g t i) -> b t g i", b=GROUPS, t=PACK, i=8)
+        gains = [late[:, SLOTS * N + 8 * j : SLOTS * N + 8 * j + 1] for j in range(SLOTS)]
+        with nc.allow_non_contiguous_dma(reason="one gain to a partition"):
+            for j in range(SLOTS):
+                nc.sync.dma_start(gains[j], gain_by_slot[j // PACK, j % PACK].unsqueeze(2))
+        w2_by_slot = w2.rearrange("(b g t i) n -> b t g i n", b=GROUPS, t=PACK, i=8)
+        for j in range(SLOTS):
+            nc.sync.dma_start(late[:, N * j : N * (j + 1)], w2_by_slot[j // PACK, j % PACK])
+
+        gather(2, BANK, keep.tile([P, S], U32, name="picked2", align_bytes=64))
+        order_w4(1, w4_late[:])
 
         banks = {}
 
@@ -130,7 +145,7 @@ def tile_list_corridor_boardings_kernel(
                 banks[j, c] = psum.tile([P, BANK], F32, name="bank", tag="bank")
             nc.tensor.matmul_mx(
                 banks[j, c][:],
-                lhsT=w4[:, a, 2 * P * j : 2 * P * (j + 1)].bitcast(FP4X4),
+                lhsT=w4[j // PACK][:, a, 2 * P * (j % PACK) : 2 * P * (j % PACK + 1)].bitcast(FP4X4),
                 lhsT_scale=w4s[:, a, P * j : P * (j + 1)],
                 rhs=picked[a][:, BANK * c : BANK * (c + 1)].bitcast(FP8X4),
                 rhs_scale=planes[a][:, BANK * c : BANK * (c + 1)],
@@ -138,20 +153,14 @@ def tile_list_corridor_boardings_kernel(
                 stop=(a == PASSES - 1),
             )
 
-        EARLY = 4
-        for a in range(PASSES - 1):
-            for j in range(EARLY):
-                for c in range(2):
-                    first_product(j, c, a)
-
         w2_codes = keep.tile([P, GROUPS, N], U32, name="w2_codes", align_bytes=64)
         w2_scales = keep.tile([P, GROUPS, N], U8, name="w2_scales", align_bytes=64)
         w2_woven = keep.tile([P, GROUPS, N, PACK], BF16, name="w2_woven", align_bytes=64)
 
         def weave_w2(b):
             nc.scalar.copy(
-                w2_woven[:, b].rearrange("p (c i) t -> p c t i", i=4),
-                late[:, PACK * N * b : PACK * N * (b + 1)].rearrange("p (t c i) -> p c t i", t=PACK, i=4),
+                w2_woven[:, b].rearrange("p (c i) t -> p c t i", i=2),
+                late[:, PACK * N * b : PACK * N * (b + 1)].rearrange("p (t c i) -> p c t i", t=PACK, i=2),
             )
 
         def quantize_w2():
@@ -167,7 +176,7 @@ def tile_list_corridor_boardings_kernel(
 
         def features(j):
             for c in range(2):
-                for a in range(PASSES - 1 if j < EARLY else 0, PASSES):
+                for a in range(PASSES):
                     first_product(j, c, a)
             h = h_tiles[j % H_TILES]
             nc.scalar.copy(h[:, 0:BANK], banks[j, 0][:])
@@ -191,9 +200,11 @@ def tile_list_corridor_boardings_kernel(
 
         def add_gain(j):
             for lo, hi in pieces(j):
-                nc.scalar.activation(
-                    poly[j // PACK][:, j % PACK, lo:hi], inner[j][:, lo:hi], ACT.Identity, bias=gains[j], scale=gains[j]
-                )
+                target = poly[j // PACK][:, j % PACK, lo:hi]
+                if j in GAIN_ON_VECTOR:
+                    nc.vector.tensor_scalar(target, inner[j][:, lo:hi], 1.0, gains[j], ADD, MULT)
+                else:
+                    nc.scalar.activation(target, inner[j][:, lo:hi], ACT.Identity, bias=gains[j], scale=gains[j])
 
         z_codes = keep.tile([P, GROUPS, LINES], U32, name="z_codes", align_bytes=64)
         z_scales = keep.tile([P, GROUPS, LINES], U8, name="z_scales", align_bytes=64)
@@ -201,9 +212,9 @@ def tile_list_corridor_boardings_kernel(
 
         def weave_z(b, cols):
             nc.vector.tensor_tensor(
-                woven[:, b, cols].rearrange("p (c i) t -> p c t i", i=4),
-                poly[b][:, :, cols].rearrange("p t (c i) -> p c t i", i=4),
-                gate[b][:, :, cols].rearrange("p t (c i) -> p c t i", i=4),
+                woven[:, b, cols].rearrange("p (c i) t -> p c t i", i=2),
+                poly[b][:, :, cols].rearrange("p t (c i) -> p c t i", i=2),
+                gate[b][:, :, cols].rearrange("p t (c i) -> p c t i", i=2),
                 MULT,
             )
 
@@ -213,19 +224,21 @@ def tile_list_corridor_boardings_kernel(
             )
 
         features(0)
+        features(1)
         for j in range(SLOTS):
+            if j + AHEAD < SLOTS:
+                features(j + AHEAD)
             look_up(j)
-            if j + 1 < SLOTS:
-                features(j + 1)
             if j > 0:
                 add_gain(j - 1)
             if j == PACK:
                 weave_z(0, slice(0, LINES))
-            if j in (2, 4):
-                weave_w2(j // 2 - 1)
-            if j == 4:
-                quantize_w2()
+            if j in (4, 5):
+                weave_w2(j - 4)
+            if j == 5:
                 quantize_z(0, slice(0, LINES))
+            if j == 6:
+                quantize_w2()
         add_gain(SLOTS - 1)
 
         def second_product(target, n, b, cols):

@@ -22,12 +22,10 @@ K_PASS = P * PACK
 PASSES = K // K_PASS
 GROUPS = H // K_PASS
 BANK = 512
-WINDOW = 2048
+WINDOW = 1024
 HALF = LINES // 2
-H_TILES = 6
 SLOTS = GROUPS * PACK
-AHEAD = 2
-GAIN_ON_VECTOR = (0, 1, 2)
+GAIN_ON_VECTOR = (7,)
 
 
 def tile_list_corridor_boardings_kernel(
@@ -38,12 +36,15 @@ def tile_list_corridor_boardings_kernel(
         keep = ctx.enter_context(tc.tile_pool(name="keep", bufs=1))
         ring = ctx.enter_context(tc.tile_pool(name="ring", bufs=2))
         shared = ctx.enter_context(tc.tile_pool(name="shared", bufs=1))
+        last = ctx.enter_context(tc.tile_pool(name="last", bufs=1))
+        rows = ctx.enter_context(tc.tile_pool(name="rows", bufs=1))
+        moving = ctx.enter_context(tc.tile_pool(name="moving", bufs=1))
         psum = ctx.enter_context(tc.psum_pool(name="psum", bufs=8))
 
         stops = keep.tile([P, S // 16], U16, name="stops")
         nc.sync.dma_start(stops[:], offs)
 
-        scale_window = keep.tile([P, T], U8, name="scale_window", tag="scale_window")
+        scale_window = last.tile([P, T], U8, name="scale_window", offset=4 * T - T // 2)
         scale_rows = tab_scales.bitcast(I32).rearrange("a q w -> (a q) w")
         row_base = (96, 112, 16)
         nc.sync.dma_start(scale_window[96:P, :].bitcast(I32), scale_rows[0:32])
@@ -51,33 +52,31 @@ def tile_list_corridor_boardings_kernel(
         for lo, hi in ((0, 16), (32, 64), (64, 96)):
             nc.vector.memset(scale_window[lo:hi, :].bitcast(I32), 0)
 
-        lists = []
-        for name, src in (("origin", pos1), ("transfer", pos2), ("dest", pos3)):
-            tile = keep.tile([P, LINES // 16], U16, name=name)
-            nc.sync.dma_start(tile[:], src)
-            lists.append(tile)
-        origin, transfer, dest = lists
-
         table = {}
 
         def load_table(a, tile):
             table[a] = tile
             nc.sync.dma_start(tile[:], tab_words[a].rearrange("p t i -> p (t i)").bitcast(I32))
 
+        lists = []
+        for name, src in (("origin", pos1), ("transfer", pos2), ("dest", pos3)):
+            tile = keep.tile([P, LINES // 16], U16, name=name)
+            nc.sync.dma_start(tile[:], src)
+            lists.append(tile)
+        origin, transfer, dest = lists
         w4_by_group = w4_words.bitcast(I32).rearrange("a p (b w) -> b p a w", b=GROUPS)
-        w4 = [keep.tile([P, PASSES, 2 * K_PASS], U8, name=f"w4_{b}", align_bytes=64) for b in range(GROUPS)]
+        w4 = {}
 
-        def order_w4(b, raw):
+        def order_w4(b, raw, tile):
+            w4[b] = tile
             nc.vector.tensor_copy(
-                w4[b][:].bitcast(I32).rearrange("p a (t g w) -> p a t g w", t=PACK, w=4),
-                raw.rearrange("p (a g t w) -> p a t g w", a=PASSES, t=PACK, w=4),
+                tile[:].bitcast(I32).rearrange("p a (t g w) -> p a t g w", t=PACK, w=4),
+                raw[:].rearrange("p a (g t w) -> p a t g w", t=PACK, w=4),
             )
 
-        W4_WORDS = PASSES * K_PASS // 2
-        w4_raw = keep.tile([P, W4_WORDS], I32, name="w4_raw")
-        nc.sync.dma_start(w4_raw[:].rearrange("p (a w) -> p a w", a=PASSES), w4_by_group[0])
-        load_table(0, keep.tile([P, T], I32, name="table0", tag="table0", align_bytes=64))
-        load_table(1, shared.tile([P, T], I32, name="table1", offset=0))
+        w4_raw = keep.tile([P, PASSES, K_PASS // 2], I32, name="w4_raw")
+        nc.sync.dma_start(w4_raw[:], w4_by_group[0])
+        load_table(0, shared.tile([P, T], I32, name="table0", offset=0))
 
         w4s_raw = keep.tile([P, PASSES, H // 4], I32, name="w4s_raw")
         nc.gpsimd.memset(w4s_raw[:], 0)
@@ -92,20 +91,28 @@ def tile_list_corridor_boardings_kernel(
         warm_out = keep.tile([P, 1], F32, name="warm_out")
         nc.scalar.activation(warm_out[:], warm[:], ACT.Sigmoid)
 
-        h_tiles = [keep.tile([P, WINDOW], F32, name=f"h{x}") for x in range(H_TILES)]
+        ones = keep.tile([P, HALF], F32, name="ones")
+        nc.vector.memset(ones[:], 1.0)
+        h_tiles = [rows.tile([P, WINDOW], F32, name=f"h{x}", offset=4 * WINDOW * x) for x in range(SLOTS)]
         picked_scales = keep.tile([P, S], U8, name="picked_scales")
         nc.vector.tensor_copy(picked_scales[:], scale_window[:].indirect(stops[:]))
-        planes = [keep.tile([P, S], U8, name=f"plane{a}", align_bytes=64) for a in range(PASSES)]
-        for a in range(PASSES):
-            nc.vector.memset(planes[a][:].bitcast(I32), 0)
+        planes = {}
 
-        for x in range(4 * PASSES):
-            a, q = divmod(x, 4)
+        def clear_plane(a, tile):
+            planes[a] = tile
+            nc.vector.memset(tile[:].bitcast(I32), 0)
+
+        def move_rows(queue, a, q):
             first = row_base[a] + 4 * q
-            nc.sync.dma_start(planes[a][32 * q : 32 * q + 4, :].bitcast(I32), picked_scales[first : first + 4, :].bitcast(I32))
-            if x == 5:
-                load_table(2, keep.tile([P, T], I32, name="table2", tag="scale_window"))
-        order_w4(0, w4_raw[:])
+            queue.dma_start(planes[a][32 * q : 32 * q + 4, :].bitcast(I32), picked_scales[first : first + 4, :].bitcast(I32))
+
+        for a in range(PASSES):
+            clear_plane(a, keep.tile([P, S], U8, name=f"plane{a}", align_bytes=64))
+        for x in range(4 * PASSES):
+            move_rows(nc.sync, *divmod(x, 4))
+            if x in (3, 7):
+                later = 1 + x // 4
+                load_table(later, last.tile([P, T], I32, name=f"table{later}", offset=4 * T * (later - 1)))
 
         picked = {}
 
@@ -115,17 +122,18 @@ def tile_list_corridor_boardings_kernel(
                 offsets = stops[:, lo // 16 : (lo + width) // 16]
                 nc.vector.tensor_copy(picked[a][:, lo : lo + width], table[a][:].bitcast(U32).indirect(offsets))
 
-        gather(0, S, keep.tile([P, S], U32, name="picked0", align_bytes=64))
+        gather(0, S, moving.tile([P, S], U32, name="picked0", offset=0 * 4 * S, align_bytes=64))
+        order_w4(0, w4_raw, keep.tile([P, PASSES, 2 * K_PASS], U8, name="w4_0", align_bytes=64))
 
-        w4s = keep.tile([P, PASSES, H], U8, name="w4s", tag="table0", align_bytes=64)
+        w4s = shared.tile([P, PASSES, H], U8, name="w4s", offset=4 * SLOTS * (N + 8) + 2 * PASSES * K_PASS, align_bytes=64)
         nc.vector.tensor_copy(
             w4s[:].bitcast(I32).rearrange("p a (b t g w) -> p (a b) t g w", b=GROUPS, t=PACK, w=2),
             w4s_raw[:].rearrange("p a (b g t w) -> p (a b) t g w", b=GROUPS, t=PACK, w=2),
         )
-        gather(1, BANK, keep.tile([P, S], U32, name="picked1", align_bytes=64))
+        gather(1, S, moving.tile([P, S], U32, name="picked1", offset=1 * 4 * S, align_bytes=64))
         late = shared.tile([P, SLOTS * (N + 8)], F32, name="late", offset=0)
-        w4_late = shared.tile([P, W4_WORDS], I32, name="w4_late", offset=4 * SLOTS * (N + 8))
-        nc.sync.dma_start(w4_late[:].rearrange("p (a w) -> p a w", a=PASSES), w4_by_group[1])
+        w4_late = shared.tile([P, PASSES, K_PASS // 2], I32, name="w4_late", offset=4 * SLOTS * (N + 8))
+        nc.sync.dma_start(w4_late[:], w4_by_group[1])
         gain_by_slot = gain.rearrange("(b g t i) -> b t g i", b=GROUPS, t=PACK, i=8)
         gains = [late[:, SLOTS * N + 8 * j : SLOTS * N + 8 * j + 1] for j in range(SLOTS)]
         with nc.allow_non_contiguous_dma(reason="one gain to a partition"):
@@ -135,8 +143,8 @@ def tile_list_corridor_boardings_kernel(
         for j in range(SLOTS):
             nc.sync.dma_start(late[:, N * j : N * (j + 1)], w2_by_slot[j // PACK, j % PACK])
 
-        gather(2, BANK, keep.tile([P, S], U32, name="picked2", align_bytes=64))
-        order_w4(1, w4_late[:])
+        gather(2, BANK, moving.tile([P, S], U32, name="picked2", offset=14 * S, align_bytes=64))
+        order_w4(1, w4_late, last.tile([P, PASSES, 2 * K_PASS], U8, name="w4_1", offset=4 * T, align_bytes=64))
 
         banks = {}
 
@@ -155,7 +163,7 @@ def tile_list_corridor_boardings_kernel(
 
         w2_codes = keep.tile([P, GROUPS, N], U32, name="w2_codes", align_bytes=64)
         w2_scales = keep.tile([P, GROUPS, N], U8, name="w2_scales", align_bytes=64)
-        w2_woven = keep.tile([P, GROUPS, N, PACK], BF16, name="w2_woven", align_bytes=64)
+        w2_woven = rows.tile([P, GROUPS, N, PACK], BF16, name="w2_woven", offset=4 * WINDOW, align_bytes=64)
 
         def weave_w2(b):
             nc.scalar.copy(
@@ -170,33 +178,40 @@ def tile_list_corridor_boardings_kernel(
             for lo, hi in ((0, 512), (512, 768)):
                 nc.vector.quantize_mx(codes[:, lo:hi].bitcast(FP8X4), scales[:, lo:hi], flat[:, PACK * lo : PACK * hi])
 
-        gate = [keep.tile([P, PACK, LINES], F32, name=f"gate{b}") for b in range(GROUPS)]
-        poly = [keep.tile([P, PACK, LINES], F32, name=f"poly{b}") for b in range(GROUPS)]
+        gates = moving.tile([P, GROUPS, PACK, LINES], F32, name="gates", offset=0)
+        polys = moving.tile([P, GROUPS, PACK, LINES], F32, name="polys", offset=16 * S)
+        gate = [gates[:, b] for b in range(GROUPS)]
+        poly = [polys[:, b] for b in range(GROUPS)]
         inner = {}
+
+        def empty_bank(j, c):
+            target = h_tiles[j][:, BANK * c : BANK * (c + 1)]
+            if (j, c) == (0, 1):
+                nc.vector.tensor_copy(target, banks[j, c][:])
+            else:
+                nc.scalar.copy(target, banks[j, c][:])
 
         def features(j):
             for c in range(2):
                 for a in range(PASSES):
                     first_product(j, c, a)
-            h = h_tiles[j % H_TILES]
-            nc.scalar.copy(h[:, 0:BANK], banks[j, 0][:])
-            if j == 0:
-                nc.vector.tensor_copy(h[:, BANK:S], banks[j, 1][:])
-            else:
-                nc.scalar.copy(h[:, BANK:S], banks[j, 1][:])
+                empty_bank(j, c)
+
+        halves = ((0, HALF), (HALF, LINES))
 
         def pieces(j):
-            return ((0, HALF), (HALF, LINES)) if j == SLOTS - 1 else ((0, LINES),)
+            return halves if j == SLOTS - 1 else ((0, LINES),)
 
-        def look_up(j):
-            h = h_tiles[j % H_TILES]
+        def pick_origin(j):
+            nc.scalar.activation(gate[j // PACK][:, j % PACK, :], h_tiles[j][:].indirect(origin[:]), ACT.Sigmoid)
+
+        def pick_inner(j):
             one_d = ring.tile([P, LINES], F32, name="one_d")
-            nc.vector.tensor_scalar(one_d[:], h[:].indirect(dest[:]), 1.0, 1.0, MULT, ADD)
-            nc.scalar.activation(gate[j // PACK][:, j % PACK, :], h[:].indirect(origin[:]), ACT.Sigmoid)
-            inner[j] = ring.tile([P, LINES], F32, name="inner", bufs=3)
-            for lo, hi in pieces(j):
-                offsets = transfer[:, lo // 16 : hi // 16]
-                nc.vector.tensor_tensor(inner[j][:, lo:hi], h[:].indirect(offsets), one_d[:, lo:hi], MULT)
+            inner[j] = keep.tile([P, LINES], F32, name=f"inner{j}")
+            for lo, hi in halves:
+                nc.vector.tensor_tensor(one_d[:, lo:hi], h_tiles[j][:].indirect(dest[:, lo // 16 : hi // 16]), ones[:], ADD)
+            for lo, hi in halves:
+                nc.vector.tensor_tensor(inner[j][:, lo:hi], h_tiles[j][:].indirect(transfer[:, lo // 16 : hi // 16]), one_d[:, lo:hi], MULT)
 
         def add_gain(j):
             for lo, hi in pieces(j):
@@ -223,23 +238,27 @@ def tile_list_corridor_boardings_kernel(
                 z_codes[:, b, cols].bitcast(FP8X4), z_scales[:, b, cols], woven[:, b, cols].rearrange("p m t -> p (m t)")
             )
 
-        features(0)
-        features(1)
+        ahead = [(0, 0), (1, 0), (0, 1), (1, 1), (2, 0), (2, 1), (3, 0), (3, 1)]
+        for a in range(PASSES - 1):
+            for j, c in ahead:
+                first_product(j, c, a)
+        for j, c in sorted(ahead, key=lambda jc: jc[1]):
+            first_product(j, c, PASSES - 1)
+        for j, c in ahead:
+            empty_bank(j, c)
+        for j in range(PACK, SLOTS):
+            features(j)
         for j in range(SLOTS):
-            if j + AHEAD < SLOTS:
-                features(j + AHEAD)
-            look_up(j)
-            if j > 0:
-                add_gain(j - 1)
+            pick_inner(j)
+            pick_origin(j)
+            add_gain(j)
             if j == PACK:
                 weave_z(0, slice(0, LINES))
             if j in (4, 5):
                 weave_w2(j - 4)
             if j == 5:
                 quantize_z(0, slice(0, LINES))
-            if j == 6:
-                quantize_w2()
-        add_gain(SLOTS - 1)
+        quantize_w2()
 
         def second_product(target, n, b, cols):
             nc.tensor.matmul_mx(

@@ -25,7 +25,7 @@ BANK = 512
 WINDOW = 1024
 HALF = LINES // 2
 SLOTS = GROUPS * PACK
-GAIN_ON_VECTOR = (7,)
+GAIN_ON_VECTOR = ()
 
 
 def tile_list_corridor_boardings_kernel(
@@ -91,7 +91,7 @@ def tile_list_corridor_boardings_kernel(
         warm_out = keep.tile([P, 1], F32, name="warm_out")
         nc.scalar.activation(warm_out[:], warm[:], ACT.Sigmoid)
 
-        ones = keep.tile([P, HALF], F32, name="ones")
+        ones = keep.tile([P, LINES], F32, name="ones")
         nc.vector.memset(ones[:], 1.0)
         h_tiles = [rows.tile([P, WINDOW], F32, name=f"h{x}", offset=4 * WINDOW * x) for x in range(SLOTS)]
         picked_scales = keep.tile([P, S], U8, name="picked_scales")
@@ -143,7 +143,7 @@ def tile_list_corridor_boardings_kernel(
         for j in range(SLOTS):
             nc.sync.dma_start(late[:, N * j : N * (j + 1)], w2_by_slot[j // PACK, j % PACK])
 
-        gather(2, BANK, moving.tile([P, S], U32, name="picked2", offset=14 * S, align_bytes=64))
+        gather(2, BANK, moving.tile([P, S], U32, name="picked2", offset=2 * 4 * S, align_bytes=64))
         order_w4(1, w4_late, last.tile([P, PASSES, 2 * K_PASS], U8, name="w4_1", offset=4 * T, align_bytes=64))
 
         banks = {}
@@ -178,8 +178,8 @@ def tile_list_corridor_boardings_kernel(
             for lo, hi in ((0, 512), (512, 768)):
                 nc.vector.quantize_mx(codes[:, lo:hi].bitcast(FP8X4), scales[:, lo:hi], flat[:, PACK * lo : PACK * hi])
 
-        gates = moving.tile([P, GROUPS, PACK, LINES], F32, name="gates", offset=0)
-        polys = moving.tile([P, GROUPS, PACK, LINES], F32, name="polys", offset=16 * S)
+        gates = keep.tile([P, GROUPS, PACK, LINES], F32, name="gates")
+        polys = moving.tile([P, GROUPS, PACK, LINES], F32, name="polys", offset=0)
         gate = [gates[:, b] for b in range(GROUPS)]
         poly = [polys[:, b] for b in range(GROUPS)]
         inner = {}
@@ -208,9 +208,8 @@ def tile_list_corridor_boardings_kernel(
         def pick_inner(j):
             one_d = ring.tile([P, LINES], F32, name="one_d")
             inner[j] = keep.tile([P, LINES], F32, name=f"inner{j}")
-            for lo, hi in halves:
-                nc.vector.tensor_tensor(one_d[:, lo:hi], h_tiles[j][:].indirect(dest[:, lo // 16 : hi // 16]), ones[:], ADD)
-            for lo, hi in halves:
+            nc.vector.tensor_tensor(one_d[:], h_tiles[j][:].indirect(dest[:]), ones[:], ADD)
+            for lo, hi in pieces(j):
                 nc.vector.tensor_tensor(inner[j][:, lo:hi], h_tiles[j][:].indirect(transfer[:, lo // 16 : hi // 16]), one_d[:, lo:hi], MULT)
 
         def add_gain(j):
@@ -239,11 +238,9 @@ def tile_list_corridor_boardings_kernel(
             )
 
         ahead = [(0, 0), (1, 0), (0, 1), (1, 1), (2, 0), (2, 1), (3, 0), (3, 1)]
-        for a in range(PASSES - 1):
+        for a in range(PASSES):
             for j, c in ahead:
                 first_product(j, c, a)
-        for j, c in sorted(ahead, key=lambda jc: jc[1]):
-            first_product(j, c, PASSES - 1)
         for j, c in ahead:
             empty_bank(j, c)
         for j in range(PACK, SLOTS):

@@ -46,10 +46,10 @@ def tile_list_corridor_boardings_kernel(
 
         scale_window = last.tile([P, T], U8, name="scale_window", offset=4 * T - T // 2)
         scale_rows = tab_scales.bitcast(I32).rearrange("a q w -> (a q) w")
-        row_base = (96, 112, 16)
+        row_base = (96, 112, 48)
         nc.sync.dma_start(scale_window[96:P, :].bitcast(I32), scale_rows[0:32])
-        nc.sync.dma_start(scale_window[16:32, :].bitcast(I32), scale_rows[32:48])
-        for lo, hi in ((0, 16), (32, 64), (64, 96)):
+        nc.sync.dma_start(scale_window[48:64, :].bitcast(I32), scale_rows[32:48])
+        for lo, hi in ((0, 48), (64, 96)):
             nc.vector.memset(scale_window[lo:hi, :].bitcast(I32), 0)
 
         table = {}
@@ -74,7 +74,7 @@ def tile_list_corridor_boardings_kernel(
                 raw[:].rearrange("p a (g t w) -> p a t g w", t=PACK, w=4),
             )
 
-        w4_raw = keep.tile([P, PASSES, K_PASS // 2], I32, name="w4_raw")
+        w4_raw = keep.tile([P, PASSES, K_PASS // 2], I32, name="w4_raw", tag="w4_raw")
         nc.sync.dma_start(w4_raw[:], w4_by_group[0])
         load_table(0, shared.tile([P, T], I32, name="table0", offset=0))
 
@@ -91,8 +91,6 @@ def tile_list_corridor_boardings_kernel(
         warm_out = keep.tile([P, 1], F32, name="warm_out")
         nc.scalar.activation(warm_out[:], warm[:], ACT.Sigmoid)
 
-        ones = keep.tile([P, LINES], F32, name="ones")
-        nc.vector.memset(ones[:], 1.0)
         h_tiles = [rows.tile([P, WINDOW], F32, name=f"h{x}", offset=4 * WINDOW * x) for x in range(SLOTS)]
         picked_scales = keep.tile([P, S], U8, name="picked_scales")
         nc.vector.tensor_copy(picked_scales[:], scale_window[:].indirect(stops[:]))
@@ -130,6 +128,8 @@ def tile_list_corridor_boardings_kernel(
             w4s[:].bitcast(I32).rearrange("p a (b t g w) -> p (a b) t g w", b=GROUPS, t=PACK, w=2),
             w4s_raw[:].rearrange("p a (b g t w) -> p (a b) t g w", b=GROUPS, t=PACK, w=2),
         )
+        ones = keep.tile([P, LINES], F32, name="ones", tag="w4_raw")
+        nc.vector.memset(ones[:], 1.0)
         gather(1, S, moving.tile([P, S], U32, name="picked1", offset=1 * 4 * S, align_bytes=64))
         late = shared.tile([P, SLOTS * (N + 8)], F32, name="late", offset=0)
         w4_late = shared.tile([P, PASSES, K_PASS // 2], I32, name="w4_late", offset=4 * SLOTS * (N + 8))
@@ -165,18 +165,18 @@ def tile_list_corridor_boardings_kernel(
         w2_scales = keep.tile([P, GROUPS, N], U8, name="w2_scales", align_bytes=64)
         w2_woven = rows.tile([P, GROUPS, N, PACK], BF16, name="w2_woven", offset=4 * WINDOW, align_bytes=64)
 
-        def weave_w2(b):
+        def weave_w2(b, lo, hi):
+            by_slot = late[:, PACK * N * b : PACK * N * (b + 1)].rearrange("p (t n) -> p t n", t=PACK)
             nc.scalar.copy(
-                w2_woven[:, b].rearrange("p (c i) t -> p c t i", i=2),
-                late[:, PACK * N * b : PACK * N * (b + 1)].rearrange("p (t c i) -> p c t i", t=PACK, i=2),
+                w2_woven[:, b, lo:hi].rearrange("p (c i) t -> p c t i", i=2),
+                by_slot[:, :, lo:hi].rearrange("p t (c i) -> p c t i", i=2),
             )
 
-        def quantize_w2():
+        def quantize_w2(lo, hi):
             flat = w2_woven[:].rearrange("p b n t -> p (b n t)")
             codes = w2_codes[:].rearrange("p b n -> p (b n)")
             scales = w2_scales[:].rearrange("p b n -> p (b n)")
-            for lo, hi in ((0, 512), (512, 768)):
-                nc.vector.quantize_mx(codes[:, lo:hi].bitcast(FP8X4), scales[:, lo:hi], flat[:, PACK * lo : PACK * hi])
+            nc.vector.quantize_mx(codes[:, lo:hi].bitcast(FP8X4), scales[:, lo:hi], flat[:, PACK * lo : PACK * hi])
 
         gates = keep.tile([P, GROUPS, PACK, LINES], F32, name="gates")
         polys = moving.tile([P, GROUPS, PACK, LINES], F32, name="polys", offset=0)
@@ -251,11 +251,13 @@ def tile_list_corridor_boardings_kernel(
             add_gain(j)
             if j == PACK:
                 weave_z(0, slice(0, LINES))
-            if j in (4, 5):
-                weave_w2(j - 4)
+            if j == 4:
+                weave_w2(0, 0, N)
             if j == 5:
+                weave_w2(1, 0, P)
                 quantize_z(0, slice(0, LINES))
-        quantize_w2()
+        weave_w2(1, P, N)
+        quantize_w2(0, N + P)
 
         def second_product(target, n, b, cols):
             nc.tensor.matmul_mx(
@@ -279,6 +281,8 @@ def tile_list_corridor_boardings_kernel(
             result = keep.tile([P, classes, P], F32, name=f"result{u}")
             if u + 1 < len(runs):
                 weave_z(1, runs[u + 1])
+                if u == 0:
+                    quantize_w2(N + P, GROUPS * N)
                 quantize_z(1, cols)
                 sums = psum.tile([P, BANK], F32, name="bank", tag="bank")
                 for n in range(classes):

@@ -52,18 +52,19 @@ def tile_list_corridor_boardings_kernel(
         for lo, hi in ((0, 48), (64, 96)):
             nc.vector.memset(scale_window[lo:hi, :].bitcast(I32), 0)
 
+        w4s_raw = keep.tile([P, PASSES, H // 4], I32, name="w4s_raw")
+        for q in range(4):
+            nc.sync.dma_start(
+                w4s_raw[32 * q : 32 * q + 4],
+                w4_scales[:, 4 * q : 4 * q + 4, :].bitcast(I32).rearrange("a r w -> r a w"),
+            )
+
         table = {}
 
         def load_table(a, tile):
             table[a] = tile
             nc.sync.dma_start(tile[:], tab_words[a].rearrange("p t i -> p (t i)").bitcast(I32))
 
-        lists = []
-        for name, src in (("origin", pos1), ("transfer", pos2), ("dest", pos3)):
-            tile = keep.tile([P, LINES // 16], U16, name=name)
-            nc.sync.dma_start(tile[:], src)
-            lists.append(tile)
-        origin, transfer, dest = lists
         w4_by_group = w4_words.bitcast(I32).rearrange("a p (b w) -> b p a w", b=GROUPS)
         w4 = {}
 
@@ -76,15 +77,13 @@ def tile_list_corridor_boardings_kernel(
 
         w4_raw = keep.tile([P, PASSES, K_PASS // 2], I32, name="w4_raw", tag="w4_raw")
         nc.sync.dma_start(w4_raw[:], w4_by_group[0])
+        lists = []
+        for name, src in (("origin", pos1), ("transfer", pos2), ("dest", pos3)):
+            tile = keep.tile([P, LINES // 16], U16, name=name)
+            nc.sync.dma_start(tile[:], src)
+            lists.append(tile)
+        origin, transfer, dest = lists
         load_table(0, shared.tile([P, T], I32, name="table0", offset=0))
-
-        w4s_raw = keep.tile([P, PASSES, H // 4], I32, name="w4s_raw")
-        nc.gpsimd.memset(w4s_raw[:], 0)
-        for q in range(4):
-            nc.gpsimd.dma_start(
-                w4s_raw[32 * q : 32 * q + 4],
-                w4_scales[:, 4 * q : 4 * q + 4, :].bitcast(I32).rearrange("a r w -> r a w"),
-            )
 
         warm = keep.tile([P, 1], F32, name="warm")
         nc.vector.memset(warm[:], 0.0)
@@ -112,6 +111,15 @@ def tile_list_corridor_boardings_kernel(
                 later = 1 + x // 4
                 load_table(later, last.tile([P, T], I32, name=f"table{later}", offset=4 * T * (later - 1)))
 
+        w4s = keep.tile([P, PASSES, H], U8, name="w4s", align_bytes=64)
+        nc.vector.memset(w4s[:].bitcast(I32), 0)
+        for q in range(4):
+            live = slice(32 * q, 32 * q + 4)
+            nc.vector.tensor_copy(
+                w4s[live].bitcast(I32).rearrange("p a (b t g w) -> p (a b) t g w", b=GROUPS, t=PACK, w=2),
+                w4s_raw[live].rearrange("p a (b g t w) -> p (a b) t g w", b=GROUPS, t=PACK, w=2),
+            )
+
         picked = {}
 
         def gather(a, width, tile):
@@ -123,11 +131,6 @@ def tile_list_corridor_boardings_kernel(
         gather(0, S, moving.tile([P, S], U32, name="picked0", offset=0 * 4 * S, align_bytes=64))
         order_w4(0, w4_raw, keep.tile([P, PASSES, 2 * K_PASS], U8, name="w4_0", align_bytes=64))
 
-        w4s = shared.tile([P, PASSES, H], U8, name="w4s", offset=4 * SLOTS * (N + 8) + 2 * PASSES * K_PASS, align_bytes=64)
-        nc.vector.tensor_copy(
-            w4s[:].bitcast(I32).rearrange("p a (b t g w) -> p (a b) t g w", b=GROUPS, t=PACK, w=2),
-            w4s_raw[:].rearrange("p a (b g t w) -> p (a b) t g w", b=GROUPS, t=PACK, w=2),
-        )
         ones = keep.tile([P, LINES], F32, name="ones", tag="w4_raw")
         nc.vector.memset(ones[:], 1.0)
         gather(1, S, moving.tile([P, S], U32, name="picked1", offset=1 * 4 * S, align_bytes=64))

@@ -41,8 +41,13 @@ def tile_list_corridor_boardings_kernel(
         moving = ctx.enter_context(tc.tile_pool(name="moving", bufs=1))
         psum = ctx.enter_context(tc.psum_pool(name="psum", bufs=8))
 
-        stops = keep.tile([P, S // 16], U16, name="stops")
-        nc.sync.dma_start(stops[:], offs)
+        def load_list(name, src, entries):
+            tile = keep.tile([P, entries // 16], U16, name=name)
+            nc.sync.dma_start(tile[:], src)
+            return tile
+
+        stops = load_list("stops", offs, S)
+        origin = load_list("origin", pos1, LINES)
 
         scale_window = last.tile([P, T], U8, name="scale_window", offset=4 * T - T // 2)
         scale_rows = tab_scales.bitcast(I32).rearrange("a q w -> (a q) w")
@@ -51,13 +56,6 @@ def tile_list_corridor_boardings_kernel(
         nc.sync.dma_start(scale_window[48:64, :].bitcast(I32), scale_rows[32:48])
         for lo, hi in ((0, 48), (64, 96)):
             nc.vector.memset(scale_window[lo:hi, :].bitcast(I32), 0)
-
-        w4s_raw = keep.tile([P, PASSES, H // 4], I32, name="w4s_raw")
-        for q in range(4):
-            nc.sync.dma_start(
-                w4s_raw[32 * q : 32 * q + 4],
-                w4_scales[:, 4 * q : 4 * q + 4, :].bitcast(I32).rearrange("a r w -> r a w"),
-            )
 
         table = {}
 
@@ -77,13 +75,16 @@ def tile_list_corridor_boardings_kernel(
 
         w4_raw = keep.tile([P, PASSES, K_PASS // 2], I32, name="w4_raw", tag="w4_raw")
         nc.sync.dma_start(w4_raw[:], w4_by_group[0])
-        lists = []
-        for name, src in (("origin", pos1), ("transfer", pos2), ("dest", pos3)):
-            tile = keep.tile([P, LINES // 16], U16, name=name)
-            nc.sync.dma_start(tile[:], src)
-            lists.append(tile)
-        origin, transfer, dest = lists
+        w4s_raw = keep.tile([P, PASSES, H // 4], I32, name="w4s_raw")
+        for q in range(4):
+            nc.sync.dma_start(
+                w4s_raw[32 * q : 32 * q + 4],
+                w4_scales[:, 4 * q : 4 * q + 4, :].bitcast(I32).rearrange("a r w -> r a w"),
+            )
+
         load_table(0, shared.tile([P, T], I32, name="table0", offset=0))
+        transfer = load_list("transfer", pos2, LINES)
+        dest = load_list("dest", pos3, LINES)
 
         warm = keep.tile([P, 1], F32, name="warm")
         nc.vector.memset(warm[:], 0.0)
@@ -133,7 +134,7 @@ def tile_list_corridor_boardings_kernel(
 
         ones = keep.tile([P, LINES], F32, name="ones", tag="w4_raw")
         nc.vector.memset(ones[:], 1.0)
-        gather(1, S, moving.tile([P, S], U32, name="picked1", offset=1 * 4 * S, align_bytes=64))
+        gather(1, BANK, moving.tile([P, S], U32, name="picked1", offset=1 * 4 * S, align_bytes=64))
         late = shared.tile([P, SLOTS * (N + 8)], F32, name="late", offset=0)
         w4_late = shared.tile([P, PASSES, K_PASS // 2], I32, name="w4_late", offset=4 * SLOTS * (N + 8))
         nc.sync.dma_start(w4_late[:], w4_by_group[1])
@@ -300,4 +301,6 @@ def tile_list_corridor_boardings_kernel(
                         nc.vector.tensor_copy(result[:, n, :], last_sums[n][:, 0:P])
                     else:
                         nc.scalar.copy(result[:, n, :], last_sums[n][:, 0:P])
-            nc.sync.dma_start(out_by_class[:, :, cols], result[:])
+                    nc.sync.dma_start(out_by_class[:, n, cols], result[:, n, :])
+            if u + 1 < len(runs):
+                nc.sync.dma_start(out_by_class[:, :, cols], result[:])

@@ -134,7 +134,7 @@ def tile_list_corridor_boardings_kernel(
 
         ones = keep.tile([P, LINES], F32, name="ones", tag="w4_raw")
         nc.vector.memset(ones[:], 1.0)
-        gather(1, BANK, moving.tile([P, S], U32, name="picked1", offset=1 * 4 * S, align_bytes=64))
+        gather(1, S, moving.tile([P, S], U32, name="picked1", offset=1 * 4 * S, align_bytes=64))
         late = shared.tile([P, SLOTS * (N + 8)], F32, name="late", offset=0)
         w4_late = shared.tile([P, PASSES, K_PASS // 2], I32, name="w4_late", offset=4 * SLOTS * (N + 8))
         nc.sync.dma_start(w4_late[:], w4_by_group[1])
@@ -263,23 +263,27 @@ def tile_list_corridor_boardings_kernel(
         weave_w2(1, P, N)
         quantize_w2(0, N + P)
 
-        def second_product(target, n, b, cols):
+        def second_product(target, n, b, cols, start, stop):
             nc.tensor.matmul_mx(
                 target,
                 lhsT=w2_codes[:, b, P * n : P * (n + 1)].bitcast(FP8X4),
                 lhsT_scale=w2_scales[:, b, P * n : P * (n + 1)],
                 rhs=z_codes[:, b, cols].bitcast(FP8X4),
                 rhs_scale=z_scales[:, b, cols],
-                start=(b == 0),
-                stop=(b == GROUPS - 1),
+                start=start,
+                stop=stop,
             )
 
         classes = N // P
         runs = [slice(lo, lo + P) for lo in range(0, LINES, P)]
         out_by_class = out.rearrange("(n p) m -> p n m", p=P)
+        sums = [psum.tile([P, BANK], F32, name="bank", tag="bank") for cols in runs[:-1]]
         last_sums = [psum.tile([P, BANK], F32, name="bank", tag="bank") for n in range(classes)]
+        for u, cols in enumerate(runs[:-1]):
+            for n in range(classes):
+                second_product(sums[u][:, P * n : P * (n + 1)], n, 0, cols, n == 0, False)
         for n in range(classes):
-            second_product(last_sums[n][:, 0:P], n, 0, runs[-1])
+            second_product(last_sums[n][:, 0:P], n, 0, runs[-1], True, False)
         weave_z(1, runs[0])
         for u, cols in enumerate(runs):
             result = keep.tile([P, classes, P], F32, name=f"result{u}")
@@ -288,19 +292,15 @@ def tile_list_corridor_boardings_kernel(
                 if u == 0:
                     quantize_w2(N + P, GROUPS * N)
                 quantize_z(1, cols)
-                sums = psum.tile([P, BANK], F32, name="bank", tag="bank")
                 for n in range(classes):
-                    for b in range(GROUPS):
-                        second_product(sums[:, P * n : P * (n + 1)], n, b, cols)
-                nc.scalar.copy(result[:].rearrange("p n m -> p (n m)"), sums[:, 0 : classes * P])
+                    second_product(sums[u][:, P * n : P * (n + 1)], n, 1, cols, False, n == classes - 1)
+                nc.scalar.copy(result[:].rearrange("p n m -> p (n m)"), sums[u][:, 0 : classes * P])
             else:
                 quantize_z(1, cols)
                 for n in range(classes):
-                    second_product(last_sums[n][:, 0:P], n, 1, cols)
+                    second_product(last_sums[n][:, 0:P], n, 1, cols, False, True)
                     if n == 1:
                         nc.vector.tensor_copy(result[:, n, :], last_sums[n][:, 0:P])
                     else:
                         nc.scalar.copy(result[:, n, :], last_sums[n][:, 0:P])
-                    nc.sync.dma_start(out_by_class[:, n, cols], result[:, n, :])
-            if u + 1 < len(runs):
-                nc.sync.dma_start(out_by_class[:, :, cols], result[:])
+            nc.sync.dma_start(out_by_class[:, :, cols], result[:])

@@ -26,6 +26,7 @@ WINDOW = 1024
 HALF = LINES // 2
 SLOTS = GROUPS * PACK
 GAIN_ON_VECTOR = ()
+SIDE_LINES = 96
 
 
 def tile_list_corridor_boardings_kernel(
@@ -41,13 +42,8 @@ def tile_list_corridor_boardings_kernel(
         moving = ctx.enter_context(tc.tile_pool(name="moving", bufs=1))
         psum = ctx.enter_context(tc.psum_pool(name="psum", bufs=8))
 
-        def load_list(name, src, entries):
-            tile = keep.tile([P, entries // 16], U16, name=name)
-            nc.sync.dma_start(tile[:], src)
-            return tile
-
-        stops = load_list("stops", offs, S)
-        origin = load_list("origin", pos1, LINES)
+        stops = keep.tile([P, S // 16], U16, name="stops")
+        nc.sync.dma_start(stops[:], offs)
 
         scale_window = last.tile([P, T], U8, name="scale_window", offset=4 * T - T // 2)
         scale_rows = tab_scales.bitcast(I32).rearrange("a q w -> (a q) w")
@@ -56,6 +52,13 @@ def tile_list_corridor_boardings_kernel(
         nc.sync.dma_start(scale_window[48:64, :].bitcast(I32), scale_rows[32:48])
         for lo, hi in ((0, 48), (64, 96)):
             nc.vector.memset(scale_window[lo:hi, :].bitcast(I32), 0)
+
+        w4s_raw = keep.tile([P, PASSES, H // 4], I32, name="w4s_raw")
+        for q in range(4):
+            nc.sync.dma_start(
+                w4s_raw[32 * q : 32 * q + 4],
+                w4_scales[:, 4 * q : 4 * q + 4, :].bitcast(I32).rearrange("a r w -> r a w"),
+            )
 
         table = {}
 
@@ -75,23 +78,21 @@ def tile_list_corridor_boardings_kernel(
 
         w4_raw = keep.tile([P, PASSES, K_PASS // 2], I32, name="w4_raw", tag="w4_raw")
         nc.sync.dma_start(w4_raw[:], w4_by_group[0])
-        w4s_raw = keep.tile([P, PASSES, H // 4], I32, name="w4s_raw")
-        for q in range(4):
-            nc.sync.dma_start(
-                w4s_raw[32 * q : 32 * q + 4],
-                w4_scales[:, 4 * q : 4 * q + 4, :].bitcast(I32).rearrange("a r w -> r a w"),
-            )
-
+        lists = []
+        for name, src in (("origin", pos1), ("transfer", pos2), ("dest", pos3)):
+            tile = keep.tile([P, LINES // 16], U16, name=name)
+            nc.sync.dma_start(tile[:], src)
+            lists.append(tile)
+        origin, transfer, dest = lists
         load_table(0, shared.tile([P, T], I32, name="table0", offset=0))
-        transfer = load_list("transfer", pos2, LINES)
-        dest = load_list("dest", pos3, LINES)
 
         warm = keep.tile([P, 1], F32, name="warm")
         nc.vector.memset(warm[:], 0.0)
         warm_out = keep.tile([P, 1], F32, name="warm_out")
         nc.scalar.activation(warm_out[:], warm[:], ACT.Sigmoid)
 
-        h_tiles = [rows.tile([P, WINDOW], F32, name=f"h{x}", offset=4 * WINDOW * x) for x in range(SLOTS)]
+        h_tiles = [rows.tile([P, WINDOW], F32, name=f"h{x}", offset=4 * WINDOW * x) for x in range(PACK)]
+        h_tiles = h_tiles + [keep.tile([P, 2 * WINDOW], F32, name=f"h{x}") for x in range(PACK, SLOTS)]
         picked_scales = keep.tile([P, S], U8, name="picked_scales")
         nc.vector.tensor_copy(picked_scales[:], scale_window[:].indirect(stops[:]))
         planes = {}
@@ -199,7 +200,8 @@ def tile_list_corridor_boardings_kernel(
             for c in range(2):
                 for a in range(PASSES):
                     first_product(j, c, a)
-                empty_bank(j, c)
+                if j < SLOTS - 2:
+                    empty_bank(j, c)
 
         halves = ((0, HALF), (HALF, LINES))
 
@@ -212,7 +214,10 @@ def tile_list_corridor_boardings_kernel(
         def pick_inner(j):
             one_d = ring.tile([P, LINES], F32, name="one_d")
             inner[j] = keep.tile([P, LINES], F32, name=f"inner{j}")
-            nc.vector.tensor_tensor(one_d[:], h_tiles[j][:].indirect(dest[:]), ones[:], ADD)
+            if j < PACK:
+                nc.vector.tensor_tensor(one_d[:], h_tiles[j][:].indirect(dest[:]), ones[:], ADD)
+            else:
+                nc.vector.tensor_scalar(one_d[:], h_tiles[j][:].indirect(dest[:]), 1.0, 1.0, MULT, ADD)
             for lo, hi in pieces(j):
                 nc.vector.tensor_tensor(inner[j][:, lo:hi], h_tiles[j][:].indirect(transfer[:, lo // 16 : hi // 16]), one_d[:, lo:hi], MULT)
 
@@ -228,8 +233,8 @@ def tile_list_corridor_boardings_kernel(
         z_scales = keep.tile([P, GROUPS, LINES], U8, name="z_scales", align_bytes=64)
         woven = keep.tile([P, GROUPS, LINES, PACK], BF16, name="woven", align_bytes=64)
 
-        def weave_z(b, cols):
-            nc.vector.tensor_tensor(
+        def weave_z(b, cols, engine=nc.vector):
+            engine.tensor_tensor(
                 woven[:, b, cols].rearrange("p (c i) t -> p c t i", i=2),
                 poly[b][:, :, cols].rearrange("p t (c i) -> p c t i", i=2),
                 gate[b][:, :, cols].rearrange("p t (c i) -> p c t i", i=2),
@@ -253,13 +258,19 @@ def tile_list_corridor_boardings_kernel(
             pick_inner(j)
             pick_origin(j)
             add_gain(j)
-            if j == PACK:
-                weave_z(0, slice(0, LINES))
+            if j == PACK - 1:
+                for lo in range(0, 3 * SIDE_LINES, SIDE_LINES):
+                    weave_z(0, slice(lo, lo + SIDE_LINES), nc.gpsimd)
+                for later in (SLOTS - 2, SLOTS - 1):
+                    for c in range(2):
+                        empty_bank(later, c)
+            if j == SLOTS - 1:
+                weave_z(0, slice(3 * SIDE_LINES, LINES))
+                quantize_z(0, slice(0, LINES))
             if j == 4:
                 weave_w2(0, 0, N)
             if j == 5:
                 weave_w2(1, 0, P)
-                quantize_z(0, slice(0, LINES))
         weave_w2(1, P, N)
         quantize_w2(0, N + P)
 

@@ -27,6 +27,9 @@ HALF = LINES // 2
 SLOTS = GROUPS * PACK
 GAIN_ON_VECTOR = ()
 SIDE_LINES = 96
+SIDE_CLASSES = 160
+EDGE = 512
+LAST_AT = 4 * T + PASSES * H
 
 
 def tile_list_corridor_boardings_kernel(
@@ -45,7 +48,7 @@ def tile_list_corridor_boardings_kernel(
         stops = keep.tile([P, S // 16], U16, name="stops")
         nc.sync.dma_start(stops[:], offs)
 
-        scale_window = last.tile([P, T], U8, name="scale_window", offset=4 * T - T // 2)
+        scale_window = last.tile([P, T], U8, name="scale_window", offset=4 * T - EDGE)
         scale_rows = tab_scales.bitcast(I32).rearrange("a q w -> (a q) w")
         row_base = (96, 112, 48)
         nc.sync.dma_start(scale_window[96:P, :].bitcast(I32), scale_rows[0:32])
@@ -95,25 +98,21 @@ def tile_list_corridor_boardings_kernel(
         h_tiles = h_tiles + [keep.tile([P, 2 * WINDOW], F32, name=f"h{x}") for x in range(PACK, SLOTS)]
         picked_scales = keep.tile([P, S], U8, name="picked_scales")
         nc.vector.tensor_copy(picked_scales[:], scale_window[:].indirect(stops[:]))
-        planes = {}
-
-        def clear_plane(a, tile):
-            planes[a] = tile
-            nc.vector.memset(tile[:].bitcast(I32), 0)
+        plane_tile = keep.tile([P, PASSES, S], U8, name="planes", align_bytes=64)
+        nc.vector.memset(plane_tile[:].bitcast(I32), 0)
+        planes = [plane_tile[:, a] for a in range(PASSES)]
 
         def move_rows(queue, a, q):
             first = row_base[a] + 4 * q
             queue.dma_start(planes[a][32 * q : 32 * q + 4, :].bitcast(I32), picked_scales[first : first + 4, :].bitcast(I32))
 
-        for a in range(PASSES):
-            clear_plane(a, keep.tile([P, S], U8, name=f"plane{a}", align_bytes=64))
         for x in range(4 * PASSES):
             move_rows(nc.sync, *divmod(x, 4))
             if x in (3, 7):
                 later = 1 + x // 4
-                load_table(later, last.tile([P, T], I32, name=f"table{later}", offset=4 * T * (later - 1)))
+                load_table(later, last.tile([P, T], I32, name=f"table{later}", offset=LAST_AT * (later - 1)))
 
-        w4s = keep.tile([P, PASSES, H], U8, name="w4s", align_bytes=64)
+        w4s = last.tile([P, PASSES, H], U8, name="w4s", offset=4 * T, align_bytes=64)
         nc.vector.memset(w4s[:].bitcast(I32), 0)
         for q in range(4):
             live = slice(32 * q, 32 * q + 4)
@@ -149,7 +148,7 @@ def tile_list_corridor_boardings_kernel(
             nc.sync.dma_start(late[:, N * j : N * (j + 1)], w2_by_slot[j // PACK, j % PACK])
 
         gather(2, BANK, moving.tile([P, S], U32, name="picked2", offset=2 * 4 * S, align_bytes=64))
-        order_w4(1, w4_late, last.tile([P, PASSES, 2 * K_PASS], U8, name="w4_1", offset=4 * T, align_bytes=64))
+        order_w4(1, w4_late, last.tile([P, PASSES, 2 * K_PASS], U8, name="w4_1", offset=LAST_AT, align_bytes=64))
 
         banks = {}
 
@@ -258,6 +257,9 @@ def tile_list_corridor_boardings_kernel(
             pick_inner(j)
             pick_origin(j)
             add_gain(j)
+            if j == PACK - 2:
+                by_slot = late[:, 0 : PACK * N].rearrange("p (t n) -> p n t", t=PACK)
+                nc.gpsimd.tensor_scalar(w2_woven[:, 0, 0:SIDE_CLASSES], by_slot[:, 0:SIDE_CLASSES], 1.0, 0.0, MULT, ADD)
             if j == PACK - 1:
                 for lo in range(0, 3 * SIDE_LINES, SIDE_LINES):
                     weave_z(0, slice(lo, lo + SIDE_LINES), nc.gpsimd)
@@ -268,7 +270,7 @@ def tile_list_corridor_boardings_kernel(
                 weave_z(0, slice(3 * SIDE_LINES, LINES))
                 quantize_z(0, slice(0, LINES))
             if j == 4:
-                weave_w2(0, 0, N)
+                weave_w2(0, SIDE_CLASSES, N)
             if j == 5:
                 weave_w2(1, 0, P)
         weave_w2(1, P, N)

@@ -22,14 +22,16 @@ K_PASS = P * PACK
 PASSES = K // K_PASS
 GROUPS = H // K_PASS
 BANK = 512
-WINDOW = 1024
+WINDOW = 2048
 HALF = LINES // 2
 SLOTS = GROUPS * PACK
-GAIN_ON_VECTOR = ()
-SIDE_LINES = 96
-SIDE_CLASSES = 160
+SIDE_GAINS = 3
+SIDE_RUNS = 3
+SIDE_CLASSES = 256
 EDGE = 512
 LAST_AT = 4 * T + PASSES * H
+W4_LATE_AT = 4 * SLOTS * N + 512
+HELD_AT = 4 * WINDOW * (SLOTS - 2)
 
 
 def tile_list_corridor_boardings_kernel(
@@ -38,7 +40,7 @@ def tile_list_corridor_boardings_kernel(
     nc = tc.nc
     with ExitStack() as ctx:
         keep = ctx.enter_context(tc.tile_pool(name="keep", bufs=1))
-        ring = ctx.enter_context(tc.tile_pool(name="ring", bufs=2))
+        ring = ctx.enter_context(tc.tile_pool(name="ring", bufs=1))
         shared = ctx.enter_context(tc.tile_pool(name="shared", bufs=1))
         last = ctx.enter_context(tc.tile_pool(name="last", bufs=1))
         rows = ctx.enter_context(tc.tile_pool(name="rows", bufs=1))
@@ -94,8 +96,7 @@ def tile_list_corridor_boardings_kernel(
         warm_out = keep.tile([P, 1], F32, name="warm_out")
         nc.scalar.activation(warm_out[:], warm[:], ACT.Sigmoid)
 
-        h_tiles = [rows.tile([P, WINDOW], F32, name=f"h{x}", offset=4 * WINDOW * x) for x in range(PACK)]
-        h_tiles = h_tiles + [keep.tile([P, 2 * WINDOW], F32, name=f"h{x}") for x in range(PACK, SLOTS)]
+        h_tiles = [rows.tile([P, WINDOW], F32, name=f"h{x}", offset=4 * WINDOW * x) for x in range(SLOTS)]
         picked_scales = keep.tile([P, S], U8, name="picked_scales")
         nc.vector.tensor_copy(picked_scales[:], scale_window[:].indirect(stops[:]))
         plane_tile = keep.tile([P, PASSES, S], U8, name="planes", align_bytes=64)
@@ -132,20 +133,19 @@ def tile_list_corridor_boardings_kernel(
         gather(0, S, moving.tile([P, S], U32, name="picked0", offset=0 * 4 * S, align_bytes=64))
         order_w4(0, w4_raw, keep.tile([P, PASSES, 2 * K_PASS], U8, name="w4_0", align_bytes=64))
 
-        ones = keep.tile([P, LINES], F32, name="ones", tag="w4_raw")
-        nc.vector.memset(ones[:], 1.0)
         gather(1, S, moving.tile([P, S], U32, name="picked1", offset=1 * 4 * S, align_bytes=64))
-        late = shared.tile([P, SLOTS * (N + 8)], F32, name="late", offset=0)
-        w4_late = shared.tile([P, PASSES, K_PASS // 2], I32, name="w4_late", offset=4 * SLOTS * (N + 8))
+        late = shared.tile([P, SLOTS * N], F32, name="late", offset=0)
+        gain_tile = shared.tile([P, SLOTS * 8], F32, name="gain_tile", offset=4 * SLOTS * N)
+        w4_late = shared.tile([P, PASSES, K_PASS // 2], I32, name="w4_late", offset=W4_LATE_AT)
         nc.sync.dma_start(w4_late[:], w4_by_group[1])
-        gain_by_slot = gain.rearrange("(b g t i) -> b t g i", b=GROUPS, t=PACK, i=8)
-        gains = [late[:, SLOTS * N + 8 * j : SLOTS * N + 8 * j + 1] for j in range(SLOTS)]
-        with nc.allow_non_contiguous_dma(reason="one gain to a partition"):
-            for j in range(SLOTS):
-                nc.sync.dma_start(gains[j], gain_by_slot[j // PACK, j % PACK].unsqueeze(2))
         w2_by_slot = w2.rearrange("(b g t i) n -> b t g i n", b=GROUPS, t=PACK, i=8)
         for j in range(SLOTS):
             nc.sync.dma_start(late[:, N * j : N * (j + 1)], w2_by_slot[j // PACK, j % PACK])
+        gain_by_slot = gain.rearrange("(b g t i) -> b t g i", b=GROUPS, t=PACK, i=8)
+        gains = [gain_tile[:, 8 * j : 8 * j + 1] for j in range(SLOTS)]
+        with nc.allow_non_contiguous_dma(reason="one gain to a partition"):
+            for j in range(SLOTS):
+                nc.sync.dma_start(gains[j], gain_by_slot[j // PACK, j % PACK].unsqueeze(2))
 
         gather(2, BANK, moving.tile([P, S], U32, name="picked2", offset=2 * 4 * S, align_bytes=64))
         order_w4(1, w4_late, last.tile([P, PASSES, 2 * K_PASS], U8, name="w4_1", offset=LAST_AT, align_bytes=64))
@@ -165,16 +165,18 @@ def tile_list_corridor_boardings_kernel(
                 stop=(a == PASSES - 1),
             )
 
-        w2_codes = keep.tile([P, GROUPS, N], U32, name="w2_codes", align_bytes=64)
+        w2_codes = rows.tile([P, GROUPS, N], U32, name="w2_codes", offset=HELD_AT + 1024, align_bytes=64)
         w2_scales = keep.tile([P, GROUPS, N], U8, name="w2_scales", align_bytes=64)
-        w2_woven = rows.tile([P, GROUPS, N, PACK], BF16, name="w2_woven", offset=4 * WINDOW, align_bytes=64)
+        w2_woven = shared.tile([P, GROUPS, N, PACK], BF16, name="w2_woven", offset=W4_LATE_AT, align_bytes=64)
 
-        def weave_w2(b, lo, hi):
+        def weave_w2(b, lo, hi, side):
             by_slot = late[:, PACK * N * b : PACK * N * (b + 1)].rearrange("p (t n) -> p t n", t=PACK)
-            nc.scalar.copy(
-                w2_woven[:, b, lo:hi].rearrange("p (c i) t -> p c t i", i=2),
-                by_slot[:, :, lo:hi].rearrange("p t (c i) -> p c t i", i=2),
-            )
+            target = w2_woven[:, b, lo:hi].rearrange("p (c i) t -> p c t i", i=2)
+            source = by_slot[:, :, lo:hi].rearrange("p t (c i) -> p c t i", i=2)
+            if side:
+                nc.gpsimd.tensor_scalar(target, source, 1.0, 0.0, MULT, ADD)
+            else:
+                nc.scalar.copy(target, source)
 
         def quantize_w2(lo, hi):
             flat = w2_woven[:].rearrange("p b n t -> p (b n t)")
@@ -182,10 +184,9 @@ def tile_list_corridor_boardings_kernel(
             scales = w2_scales[:].rearrange("p b n -> p (b n)")
             nc.vector.quantize_mx(codes[:, lo:hi].bitcast(FP8X4), scales[:, lo:hi], flat[:, PACK * lo : PACK * hi])
 
-        gates = keep.tile([P, GROUPS, PACK, LINES], F32, name="gates")
-        polys = moving.tile([P, GROUPS, PACK, LINES], F32, name="polys", offset=0)
-        gate = [gates[:, b] for b in range(GROUPS)]
-        poly = [polys[:, b] for b in range(GROUPS)]
+        gate = [keep.tile([P, PACK, LINES], F32, name=f"gate{b}") for b in range(GROUPS)]
+        poly = [keep.tile([P, PACK, LINES], F32, name=f"poly{b}") for b in range(GROUPS)]
+        one_d = {}
         inner = {}
 
         def empty_bank(j, c):
@@ -195,100 +196,108 @@ def tile_list_corridor_boardings_kernel(
             else:
                 nc.scalar.copy(target, banks[j, c][:])
 
-        def features(j):
-            for c in range(2):
-                for a in range(PASSES):
-                    first_product(j, c, a)
-                if j < SLOTS - 2:
-                    empty_bank(j, c)
-
         halves = ((0, HALF), (HALF, LINES))
 
         def pieces(j):
-            return halves if j == SLOTS - 1 else ((0, LINES),)
+            return halves if j % PACK == PACK - 1 else ((0, LINES),)
 
         def pick_origin(j):
             nc.scalar.activation(gate[j // PACK][:, j % PACK, :], h_tiles[j][:].indirect(origin[:]), ACT.Sigmoid)
 
-        def pick_inner(j):
-            one_d = ring.tile([P, LINES], F32, name="one_d")
-            inner[j] = keep.tile([P, LINES], F32, name=f"inner{j}")
-            if j < PACK:
-                nc.vector.tensor_tensor(one_d[:], h_tiles[j][:].indirect(dest[:]), ones[:], ADD)
+        def pick_dest(j):
+            one_d[j] = ring.tile([P, LINES], F32, name=f"one_d{j}", offset=4 * LINES * j, align_bytes=64)
+            nc.vector.tensor_scalar(one_d[j][:], h_tiles[j][:].indirect(dest[:]), 1.0, 1.0, MULT, ADD)
+
+        def pick_transfer(j):
+            if 0 < j < SLOTS - 1:
+                inner[j] = rows.tile([P, LINES], F32, name=f"inner{j}", offset=4 * WINDOW * (j - 1))
             else:
-                nc.vector.tensor_scalar(one_d[:], h_tiles[j][:].indirect(dest[:]), 1.0, 1.0, MULT, ADD)
+                inner[j] = keep.tile([P, LINES], F32, name=f"inner{j}")
             for lo, hi in pieces(j):
-                nc.vector.tensor_tensor(inner[j][:, lo:hi], h_tiles[j][:].indirect(transfer[:, lo // 16 : hi // 16]), one_d[:, lo:hi], MULT)
+                nc.vector.tensor_tensor(inner[j][:, lo:hi], h_tiles[j][:].indirect(transfer[:, lo // 16 : hi // 16]), one_d[j][:, lo:hi], MULT)
 
-        def add_gain(j):
-            for lo, hi in pieces(j):
-                target = poly[j // PACK][:, j % PACK, lo:hi]
-                if j in GAIN_ON_VECTOR:
-                    nc.vector.tensor_scalar(target, inner[j][:, lo:hi], 1.0, gains[j], ADD, MULT)
-                else:
-                    nc.scalar.activation(target, inner[j][:, lo:hi], ACT.Identity, bias=gains[j], scale=gains[j])
+        def add_gain(j, lo, hi):
+            target = poly[j // PACK][:, j % PACK, lo:hi]
+            if j < SIDE_GAINS:
+                nc.gpsimd.tensor_scalar(target, inner[j][:, lo:hi], gains[j], gains[j], MULT, ADD)
+            else:
+                nc.scalar.activation(target, inner[j][:, lo:hi], ACT.Identity, bias=gains[j], scale=gains[j])
 
-        z_codes = keep.tile([P, GROUPS, LINES], U32, name="z_codes", align_bytes=64)
+        classes = N // P
+        runs = [slice(lo, lo + P) for lo in range(0, LINES, P)]
         z_scales = keep.tile([P, GROUPS, LINES], U8, name="z_scales", align_bytes=64)
-        woven = keep.tile([P, GROUPS, LINES, PACK], BF16, name="woven", align_bytes=64)
+        z_codes = {}
+        woven = {}
 
-        def weave_z(b, cols, engine=nc.vector):
+        def weave_z(b, u, tile, engine=nc.vector):
+            woven[b, u] = tile
             engine.tensor_tensor(
-                woven[:, b, cols].rearrange("p (c i) t -> p c t i", i=2),
-                poly[b][:, :, cols].rearrange("p t (c i) -> p c t i", i=2),
-                gate[b][:, :, cols].rearrange("p t (c i) -> p c t i", i=2),
+                tile[:].rearrange("p (c i) t -> p c t i", i=2),
+                poly[b][:, :, runs[u]].rearrange("p t (c i) -> p c t i", i=2),
+                gate[b][:, :, runs[u]].rearrange("p t (c i) -> p c t i", i=2),
                 MULT,
             )
 
-        def quantize_z(b, cols):
+        def quantize_z(b, u):
             nc.vector.quantize_mx(
-                z_codes[:, b, cols].bitcast(FP8X4), z_scales[:, b, cols], woven[:, b, cols].rearrange("p m t -> p (m t)")
+                z_codes[b][:, runs[u]].bitcast(FP8X4), z_scales[:, b, runs[u]], woven[b, u][:].rearrange("p m t -> p (m t)")
             )
 
         ahead = [(0, 0), (1, 0), (0, 1), (1, 1), (2, 0), (2, 1), (3, 0), (3, 1)]
         for a in range(PASSES):
             for j, c in ahead:
                 first_product(j, c, a)
-        for j, c in ahead:
+        for j, c in ahead[:4]:
             empty_bank(j, c)
         for j in range(PACK, SLOTS):
-            features(j)
-        for j in range(SLOTS):
-            pick_inner(j)
-            pick_origin(j)
-            add_gain(j)
-            if j == PACK - 2:
-                by_slot = late[:, 0 : PACK * N].rearrange("p (t n) -> p n t", t=PACK)
-                nc.gpsimd.tensor_scalar(w2_woven[:, 0, 0:SIDE_CLASSES], by_slot[:, 0:SIDE_CLASSES], 1.0, 0.0, MULT, ADD)
-            if j == PACK - 1:
-                for lo in range(0, 3 * SIDE_LINES, SIDE_LINES):
-                    weave_z(0, slice(lo, lo + SIDE_LINES), nc.gpsimd)
-                for later in (SLOTS - 2, SLOTS - 1):
-                    for c in range(2):
-                        empty_bank(later, c)
-            if j == SLOTS - 1:
-                weave_z(0, slice(3 * SIDE_LINES, LINES))
-                quantize_z(0, slice(0, LINES))
-            if j == 4:
-                weave_w2(0, SIDE_CLASSES, N)
-            if j == 5:
-                weave_w2(1, 0, P)
-        weave_w2(1, P, N)
+            for c in range(2):
+                for a in range(PASSES):
+                    first_product(j, c, a)
+        weave_w2(0, 0, N, True)
+        weave_w2(1, 0, SIDE_CLASSES, True)
+        pick_dest(0)
+        for j in range(SLOTS + 1):
+            if 1 < j + 1 < SLOTS:
+                empty_bank(j + 1, 0)
+                if j - 2 == PACK - 1:
+                    add_gain(j - 2, HALF, LINES)
+                    for u in range(SIDE_RUNS):
+                        if u == 0:
+                            tile = keep.tile([P, P, PACK], BF16, name="woven00", align_bytes=64)
+                        else:
+                            tile = ring.tile([P, P, PACK], BF16, name=f"woven0{u}", offset=4 * LINES * (PACK - 1 + u), align_bytes=64)
+                        weave_z(0, u, tile, nc.gpsimd)
+                empty_bank(j + 1, 1)
+            if j + 1 < SLOTS:
+                pick_dest(j + 1)
+            if j > 0:
+                pick_origin(j - 1)
+                for lo, hi in pieces(j - 1)[: 1 if j == PACK else 2]:
+                    add_gain(j - 1, lo, hi)
+            if j == SLOTS - 2:
+                weave_w2(1, SIDE_CLASSES, N, False)
+            if j < SLOTS:
+                pick_transfer(j)
+        z_codes[0] = ring.tile([P, LINES], U32, name="z_codes0", offset=4 * LINES * (SLOTS - 2), align_bytes=64)
+        z_codes[1] = keep.tile([P, LINES], U32, name="z_codes1", align_bytes=64)
+        for u in range(SIDE_RUNS, len(runs)):
+            weave_z(0, u, rows.tile([P, P, PACK], BF16, name=f"woven0{u}", offset=HELD_AT, align_bytes=64))
         quantize_w2(0, N + P)
+        for u in range(len(runs)):
+            quantize_z(0, u)
+        quantize_w2(N + P, GROUPS * N)
 
         def second_product(target, n, b, cols, start, stop):
             nc.tensor.matmul_mx(
                 target,
                 lhsT=w2_codes[:, b, P * n : P * (n + 1)].bitcast(FP8X4),
                 lhsT_scale=w2_scales[:, b, P * n : P * (n + 1)],
-                rhs=z_codes[:, b, cols].bitcast(FP8X4),
+                rhs=z_codes[b][:, cols].bitcast(FP8X4),
                 rhs_scale=z_scales[:, b, cols],
                 start=start,
                 stop=stop,
             )
 
-        classes = N // P
-        runs = [slice(lo, lo + P) for lo in range(0, LINES, P)]
         out_by_class = out.rearrange("(n p) m -> p n m", p=P)
         sums = [psum.tile([P, BANK], F32, name="bank", tag="bank") for cols in runs[:-1]]
         last_sums = [psum.tile([P, BANK], F32, name="bank", tag="bank") for n in range(classes)]
@@ -297,19 +306,17 @@ def tile_list_corridor_boardings_kernel(
                 second_product(sums[u][:, P * n : P * (n + 1)], n, 0, cols, n == 0, False)
         for n in range(classes):
             second_product(last_sums[n][:, 0:P], n, 0, runs[-1], True, False)
-        weave_z(1, runs[0])
+        weave_z(1, 0, keep.tile([P, P, PACK], BF16, name="woven10", align_bytes=64))
         for u, cols in enumerate(runs):
             result = keep.tile([P, classes, P], F32, name=f"result{u}")
             if u + 1 < len(runs):
-                weave_z(1, runs[u + 1])
-                if u == 0:
-                    quantize_w2(N + P, GROUPS * N)
-                quantize_z(1, cols)
+                weave_z(1, u + 1, keep.tile([P, P, PACK], BF16, name=f"woven1{u + 1}", align_bytes=64))
+                quantize_z(1, u)
                 for n in range(classes):
                     second_product(sums[u][:, P * n : P * (n + 1)], n, 1, cols, False, n == classes - 1)
                 nc.scalar.copy(result[:].rearrange("p n m -> p (n m)"), sums[u][:, 0 : classes * P])
             else:
-                quantize_z(1, cols)
+                quantize_z(1, u)
                 for n in range(classes):
                     second_product(last_sums[n][:, 0:P], n, 1, cols, False, True)
                     if n == 1:

@@ -25,9 +25,11 @@ BANK = 512
 WINDOW = 2048
 HALF = LINES // 2
 SLOTS = GROUPS * PACK
-SIDE_GAINS = 3
-SIDE_RUNS = 3
-SIDE_CLASSES = 256
+SIDE_GAINS = (0, 1, 3)
+SIDE_CLASSES = 192
+FIRST_LINES = 128
+SECOND_LINES = 192
+HELD_ON = {2: 0, 3: 0, 4: 3, 5: 3, 6: 5, 7: 5}
 EDGE = 512
 LAST_AT = 4 * T + PASSES * H
 W4_LATE_AT = 4 * SLOTS * N + 512
@@ -165,24 +167,23 @@ def tile_list_corridor_boardings_kernel(
                 stop=(a == PASSES - 1),
             )
 
-        w2_codes = rows.tile([P, GROUPS, N], U32, name="w2_codes", offset=HELD_AT + 1024, align_bytes=64)
+        w2_codes = rows.tile([P, GROUPS, N], U32, name="w2_codes", offset=HELD_AT + 2048, align_bytes=64)
         w2_scales = keep.tile([P, GROUPS, N], U8, name="w2_scales", align_bytes=64)
-        w2_woven = shared.tile([P, GROUPS, N, PACK], BF16, name="w2_woven", offset=W4_LATE_AT, align_bytes=64)
+        w2_woven = shared.tile([P, N, PACK], BF16, name="w2_woven", offset=W4_LATE_AT, align_bytes=64)
 
-        def weave_w2(b, lo, hi, side):
+        def weave_w2(b, lo, hi, target, side):
             by_slot = late[:, PACK * N * b : PACK * N * (b + 1)].rearrange("p (t n) -> p t n", t=PACK)
-            target = w2_woven[:, b, lo:hi].rearrange("p (c i) t -> p c t i", i=2)
+            target = target.rearrange("p (c i) t -> p c t i", i=2)
             source = by_slot[:, :, lo:hi].rearrange("p t (c i) -> p c t i", i=2)
             if side:
                 nc.gpsimd.tensor_scalar(target, source, 1.0, 0.0, MULT, ADD)
             else:
                 nc.scalar.copy(target, source)
 
-        def quantize_w2(lo, hi):
-            flat = w2_woven[:].rearrange("p b n t -> p (b n t)")
+        def quantize_w2(lo, hi, source):
             codes = w2_codes[:].rearrange("p b n -> p (b n)")
             scales = w2_scales[:].rearrange("p b n -> p (b n)")
-            nc.vector.quantize_mx(codes[:, lo:hi].bitcast(FP8X4), scales[:, lo:hi], flat[:, PACK * lo : PACK * hi])
+            nc.vector.quantize_mx(codes[:, lo:hi].bitcast(FP8X4), scales[:, lo:hi], source.rearrange("p n t -> p (n t)"))
 
         gate = [keep.tile([P, PACK, LINES], F32, name=f"gate{b}") for b in range(GROUPS)]
         poly = [keep.tile([P, PACK, LINES], F32, name=f"poly{b}") for b in range(GROUPS)]
@@ -196,52 +197,45 @@ def tile_list_corridor_boardings_kernel(
             else:
                 nc.scalar.copy(target, banks[j, c][:])
 
-        halves = ((0, HALF), (HALF, LINES))
-
-        def pieces(j):
-            return halves if j % PACK == PACK - 1 else ((0, LINES),)
-
-        def pick_origin(j):
-            nc.scalar.activation(gate[j // PACK][:, j % PACK, :], h_tiles[j][:].indirect(origin[:]), ACT.Sigmoid)
+        def pick_origin(j, lo=0, hi=LINES):
+            nc.scalar.activation(gate[j // PACK][:, j % PACK, lo:hi], h_tiles[j][:].indirect(origin[:, lo // 16 : hi // 16]), ACT.Sigmoid)
 
         def pick_dest(j):
             one_d[j] = ring.tile([P, LINES], F32, name=f"one_d{j}", offset=4 * LINES * j, align_bytes=64)
             nc.vector.tensor_scalar(one_d[j][:], h_tiles[j][:].indirect(dest[:]), 1.0, 1.0, MULT, ADD)
 
         def pick_transfer(j):
-            if 0 < j < SLOTS - 1:
-                inner[j] = rows.tile([P, LINES], F32, name=f"inner{j}", offset=4 * WINDOW * (j - 1))
+            if j in HELD_ON:
+                at = 4 * WINDOW * HELD_ON[j] + 4 * LINES * (j % 2)
+                inner[j] = rows.tile([P, LINES], F32, name=f"inner{j}", offset=at)
             else:
                 inner[j] = keep.tile([P, LINES], F32, name=f"inner{j}")
-            for lo, hi in pieces(j):
-                nc.vector.tensor_tensor(inner[j][:, lo:hi], h_tiles[j][:].indirect(transfer[:, lo // 16 : hi // 16]), one_d[j][:, lo:hi], MULT)
+            nc.vector.tensor_tensor(inner[j][:], h_tiles[j][:].indirect(transfer[:]), one_d[j][:], MULT)
 
-        def add_gain(j, lo, hi):
-            target = poly[j // PACK][:, j % PACK, lo:hi]
-            if j < SIDE_GAINS:
-                nc.gpsimd.tensor_scalar(target, inner[j][:, lo:hi], gains[j], gains[j], MULT, ADD)
+        def add_gain(j):
+            target = poly[j // PACK][:, j % PACK, :]
+            if j in SIDE_GAINS:
+                nc.gpsimd.tensor_scalar(target, inner[j][:], gains[j], gains[j], MULT, ADD)
             else:
-                nc.scalar.activation(target, inner[j][:, lo:hi], ACT.Identity, bias=gains[j], scale=gains[j])
+                nc.scalar.activation(target, inner[j][:], ACT.Identity, bias=gains[j], scale=gains[j])
 
         classes = N // P
         runs = [slice(lo, lo + P) for lo in range(0, LINES, P)]
         z_scales = keep.tile([P, GROUPS, LINES], U8, name="z_scales", align_bytes=64)
         z_codes = {}
-        woven = {}
 
-        def weave_z(b, u, tile, engine=nc.vector):
-            woven[b, u] = tile
+        def weave_z(b, lo, tile, engine=nc.vector):
+            cols = slice(lo, lo + tile.shape[1])
             engine.tensor_tensor(
                 tile[:].rearrange("p (c i) t -> p c t i", i=2),
-                poly[b][:, :, runs[u]].rearrange("p t (c i) -> p c t i", i=2),
-                gate[b][:, :, runs[u]].rearrange("p t (c i) -> p c t i", i=2),
+                poly[b][:, :, cols].rearrange("p t (c i) -> p c t i", i=2),
+                gate[b][:, :, cols].rearrange("p t (c i) -> p c t i", i=2),
                 MULT,
             )
 
-        def quantize_z(b, u):
-            nc.vector.quantize_mx(
-                z_codes[b][:, runs[u]].bitcast(FP8X4), z_scales[:, b, runs[u]], woven[b, u][:].rearrange("p m t -> p (m t)")
-            )
+        def quantize_z(b, lo, source):
+            cols = slice(lo, lo + source.shape[1])
+            nc.vector.quantize_mx(z_codes[b][:, cols].bitcast(FP8X4), z_scales[:, b, cols], source.rearrange("p m t -> p (m t)"))
 
         ahead = [(0, 0), (1, 0), (0, 1), (1, 1), (2, 0), (2, 1), (3, 0), (3, 1)]
         for a in range(PASSES):
@@ -253,39 +247,67 @@ def tile_list_corridor_boardings_kernel(
             for c in range(2):
                 for a in range(PASSES):
                     first_product(j, c, a)
-        weave_w2(0, 0, N, True)
-        weave_w2(1, 0, SIDE_CLASSES, True)
-        pick_dest(0)
-        for j in range(SLOTS + 1):
-            if 1 < j + 1 < SLOTS:
-                empty_bank(j + 1, 0)
-                if j - 2 == PACK - 1:
-                    add_gain(j - 2, HALF, LINES)
-                    for u in range(SIDE_RUNS):
-                        if u == 0:
-                            tile = keep.tile([P, P, PACK], BF16, name="woven00", align_bytes=64)
-                        else:
-                            tile = ring.tile([P, P, PACK], BF16, name=f"woven0{u}", offset=4 * LINES * (PACK - 1 + u), align_bytes=64)
-                        weave_z(0, u, tile, nc.gpsimd)
-                empty_bank(j + 1, 1)
-            if j + 1 < SLOTS:
-                pick_dest(j + 1)
-            if j > 0:
-                pick_origin(j - 1)
-                for lo, hi in pieces(j - 1)[: 1 if j == PACK else 2]:
-                    add_gain(j - 1, lo, hi)
-            if j == SLOTS - 2:
-                weave_w2(1, SIDE_CLASSES, N, False)
-            if j < SLOTS:
-                pick_transfer(j)
+        weave_w2(0, 0, N, w2_woven[:], True)
+
+        def empty_slot(j):
+            for c in range(2):
+                empty_bank(j, c)
+
+        def pick_pair(j):
+            for x in (j, j + 1):
+                pick_dest(x)
+            for x in (j, j + 1):
+                pick_transfer(x)
+
+        empty_slot(2)
+        empty_slot(3)
+        pick_pair(0)
+        add_gain(0)
+        add_gain(1)
+        w2_side = ring.tile([P, SIDE_CLASSES, PACK], BF16, name="w2_side", offset=0, align_bytes=64)
+        weave_w2(1, 0, SIDE_CLASSES, w2_side[:], True)
+        pick_origin(0)
+        pick_pair(2)
+        empty_slot(4)
+        pick_origin(1)
+        empty_slot(5)
+        pick_origin(2)
+        pick_origin(3, 0, HALF)
+        add_gain(2)
+        add_gain(3)
+        first = keep.tile([P, FIRST_LINES, PACK], BF16, name="woven_first", align_bytes=64)
+        weave_z(0, 0, first, nc.gpsimd)
+        pick_origin(3, HALF, LINES)
+        pick_pair(4)
+        second = ring.tile([P, SECOND_LINES, PACK], BF16, name="woven_second", offset=4 * LINES * 4, align_bytes=64)
+        weave_z(0, FIRST_LINES, second, nc.gpsimd)
+        empty_slot(6)
+        pick_origin(4)
+        empty_slot(7)
+        pick_origin(5)
+        pick_pair(6)
+        add_gain(4)
+        add_gain(5)
+        pick_origin(6)
+        pick_origin(7)
+        add_gain(6)
+        add_gain(7)
+        w2_rest = ring.tile([P, N - SIDE_CLASSES, PACK], BF16, name="w2_rest", offset=4 * LINES * 5, align_bytes=64)
+        weave_w2(1, SIDE_CLASSES, N, w2_rest[:], False)
         z_codes[0] = ring.tile([P, LINES], U32, name="z_codes0", offset=4 * LINES * (SLOTS - 2), align_bytes=64)
         z_codes[1] = keep.tile([P, LINES], U32, name="z_codes1", align_bytes=64)
-        for u in range(SIDE_RUNS, len(runs)):
-            weave_z(0, u, rows.tile([P, P, PACK], BF16, name=f"woven0{u}", offset=HELD_AT, align_bytes=64))
-        quantize_w2(0, N + P)
-        for u in range(len(runs)):
-            quantize_z(0, u)
-        quantize_w2(N + P, GROUPS * N)
+        side_lines = FIRST_LINES + SECOND_LINES
+        third = rows.tile([P, LINES - side_lines, PACK], BF16, name="woven_third", offset=HELD_AT, align_bytes=64)
+        weave_z(0, side_lines, third)
+        quantize_w2(0, 2 * P, w2_woven[:, 0 : 2 * P])
+        quantize_w2(2 * P, N, w2_woven[:, 2 * P :])
+        quantize_z(0, 0, first[:])
+        quantize_z(0, FIRST_LINES, second[:, 0:P])
+        quantize_z(0, FIRST_LINES + P, second[:, P:])
+        quantize_z(0, side_lines, third[:, 0 : P // 2])
+        quantize_z(0, side_lines + P // 2, third[:, P // 2 :])
+        quantize_w2(N, N + P, w2_side[:, 0:P])
+        quantize_w2(N + P, N + SIDE_CLASSES, w2_side[:, P:])
 
         def second_product(target, n, b, cols, start, stop):
             nc.tensor.matmul_mx(
@@ -306,17 +328,21 @@ def tile_list_corridor_boardings_kernel(
                 second_product(sums[u][:, P * n : P * (n + 1)], n, 0, cols, n == 0, False)
         for n in range(classes):
             second_product(last_sums[n][:, 0:P], n, 0, runs[-1], True, False)
-        weave_z(1, 0, keep.tile([P, P, PACK], BF16, name="woven10", align_bytes=64))
+        woven = [keep.tile([P, P, PACK], BF16, name=f"woven1{u}", align_bytes=64) for u in range(len(runs))]
+        weave_z(1, 0, woven[0])
         for u, cols in enumerate(runs):
             result = keep.tile([P, classes, P], F32, name=f"result{u}")
             if u + 1 < len(runs):
-                weave_z(1, u + 1, keep.tile([P, P, PACK], BF16, name=f"woven1{u + 1}", align_bytes=64))
-                quantize_z(1, u)
+                weave_z(1, P * (u + 1), woven[u + 1])
+                if u == 0:
+                    quantize_w2(N + SIDE_CLASSES, N + 2 * P, w2_rest[:, 0 : P // 2])
+                    quantize_w2(N + 2 * P, GROUPS * N, w2_rest[:, P // 2 :])
+                quantize_z(1, P * u, woven[u][:])
                 for n in range(classes):
                     second_product(sums[u][:, P * n : P * (n + 1)], n, 1, cols, False, n == classes - 1)
                 nc.scalar.copy(result[:].rearrange("p n m -> p (n m)"), sums[u][:, 0 : classes * P])
             else:
-                quantize_z(1, u)
+                quantize_z(1, P * u, woven[u][:])
                 for n in range(classes):
                     second_product(last_sums[n][:, 0:P], n, 1, cols, False, True)
                     if n == 1:

@@ -23,11 +23,10 @@ PASSES = K // K_PASS
 GROUPS = H // K_PASS
 BANK = 512
 WINDOW = 2048
-HALF = LINES // 2
 SLOTS = GROUPS * PACK
-SIDE_GAINS = (0, 1, 3)
-SIDE_CLASSES = 192
-FIRST_LINES = 128
+SIDE_GAINS = (0, 1)
+FIRST_CLASSES = 256
+FIRST_LINES = 192
 SECOND_LINES = 192
 HELD_ON = {2: 0, 3: 0, 4: 3, 5: 3, 6: 5, 7: 5}
 EDGE = 512
@@ -169,7 +168,7 @@ def tile_list_corridor_boardings_kernel(
 
         w2_codes = rows.tile([P, GROUPS, N], U32, name="w2_codes", offset=HELD_AT + 2048, align_bytes=64)
         w2_scales = keep.tile([P, GROUPS, N], U8, name="w2_scales", align_bytes=64)
-        w2_woven = shared.tile([P, N, PACK], BF16, name="w2_woven", offset=W4_LATE_AT, align_bytes=64)
+        w2_woven = shared.tile([P, FIRST_CLASSES, PACK], BF16, name="w2_woven", offset=W4_LATE_AT, align_bytes=64)
 
         def weave_w2(b, lo, hi, target, side):
             by_slot = late[:, PACK * N * b : PACK * N * (b + 1)].rearrange("p (t n) -> p t n", t=PACK)
@@ -197,12 +196,14 @@ def tile_list_corridor_boardings_kernel(
             else:
                 nc.scalar.copy(target, banks[j, c][:])
 
-        def pick_origin(j, lo=0, hi=LINES):
-            nc.scalar.activation(gate[j // PACK][:, j % PACK, lo:hi], h_tiles[j][:].indirect(origin[:, lo // 16 : hi // 16]), ACT.Sigmoid)
+        def pick_origin(j):
+            nc.scalar.activation(gate[j // PACK][:, j % PACK, :], h_tiles[j][:].indirect(origin[:]), ACT.Sigmoid)
 
         def pick_dest(j):
             one_d[j] = ring.tile([P, LINES], F32, name=f"one_d{j}", offset=4 * LINES * j, align_bytes=64)
             nc.vector.tensor_scalar(one_d[j][:], h_tiles[j][:].indirect(dest[:]), 1.0, 1.0, MULT, ADD)
+
+        parts = ((0, FIRST_LINES), (FIRST_LINES, LINES))
 
         def pick_transfer(j):
             if j in HELD_ON:
@@ -210,14 +211,15 @@ def tile_list_corridor_boardings_kernel(
                 inner[j] = rows.tile([P, LINES], F32, name=f"inner{j}", offset=at)
             else:
                 inner[j] = keep.tile([P, LINES], F32, name=f"inner{j}")
-            nc.vector.tensor_tensor(inner[j][:], h_tiles[j][:].indirect(transfer[:]), one_d[j][:], MULT)
+            for lo, hi in parts if j == PACK - 1 else ((0, LINES),):
+                nc.vector.tensor_tensor(inner[j][:, lo:hi], h_tiles[j][:].indirect(transfer[:, lo // 16 : hi // 16]), one_d[j][:, lo:hi], MULT)
 
-        def add_gain(j):
-            target = poly[j // PACK][:, j % PACK, :]
-            if j in SIDE_GAINS:
-                nc.gpsimd.tensor_scalar(target, inner[j][:], gains[j], gains[j], MULT, ADD)
+        def add_gain(j, lo=0, hi=LINES):
+            target = poly[j // PACK][:, j % PACK, lo:hi]
+            if j in SIDE_GAINS or (j, lo) == (PACK - 1, 0):
+                nc.gpsimd.tensor_scalar(target, inner[j][:, lo:hi], gains[j], gains[j], MULT, ADD)
             else:
-                nc.scalar.activation(target, inner[j][:], ACT.Identity, bias=gains[j], scale=gains[j])
+                nc.scalar.activation(target, inner[j][:, lo:hi], ACT.Identity, bias=gains[j], scale=gains[j])
 
         classes = N // P
         runs = [slice(lo, lo + P) for lo in range(0, LINES, P)]
@@ -247,7 +249,7 @@ def tile_list_corridor_boardings_kernel(
             for c in range(2):
                 for a in range(PASSES):
                     first_product(j, c, a)
-        weave_w2(0, 0, N, w2_woven[:], True)
+        weave_w2(0, 0, FIRST_CLASSES, w2_woven[:], True)
 
         def empty_slot(j):
             for c in range(2):
@@ -264,20 +266,21 @@ def tile_list_corridor_boardings_kernel(
         pick_pair(0)
         add_gain(0)
         add_gain(1)
-        w2_side = ring.tile([P, SIDE_CLASSES, PACK], BF16, name="w2_side", offset=0, align_bytes=64)
-        weave_w2(1, 0, SIDE_CLASSES, w2_side[:], True)
+        w2_side = ring.tile([P, N - FIRST_CLASSES, PACK], BF16, name="w2_side", offset=0, align_bytes=64)
+        weave_w2(0, FIRST_CLASSES, N, w2_side[:], True)
         pick_origin(0)
         pick_pair(2)
         empty_slot(4)
         pick_origin(1)
         empty_slot(5)
         pick_origin(2)
-        pick_origin(3, 0, HALF)
-        add_gain(2)
-        add_gain(3)
+        pick_origin(3)
+        add_gain(2, *parts[0])
+        add_gain(3, *parts[0])
         first = keep.tile([P, FIRST_LINES, PACK], BF16, name="woven_first", align_bytes=64)
         weave_z(0, 0, first, nc.gpsimd)
-        pick_origin(3, HALF, LINES)
+        add_gain(2, *parts[1])
+        add_gain(3, *parts[1])
         pick_pair(4)
         second = ring.tile([P, SECOND_LINES, PACK], BF16, name="woven_second", offset=4 * LINES * 4, align_bytes=64)
         weave_z(0, FIRST_LINES, second, nc.gpsimd)
@@ -292,22 +295,20 @@ def tile_list_corridor_boardings_kernel(
         pick_origin(7)
         add_gain(6)
         add_gain(7)
-        w2_rest = ring.tile([P, N - SIDE_CLASSES, PACK], BF16, name="w2_rest", offset=4 * LINES * 5, align_bytes=64)
-        weave_w2(1, SIDE_CLASSES, N, w2_rest[:], False)
+        w2_rest = rows.tile([P, N, PACK], BF16, name="w2_rest", offset=HELD_AT + 5120, align_bytes=64)
+        weave_w2(1, 0, N, w2_rest[:], False)
         z_codes[0] = ring.tile([P, LINES], U32, name="z_codes0", offset=4 * LINES * (SLOTS - 2), align_bytes=64)
         z_codes[1] = keep.tile([P, LINES], U32, name="z_codes1", align_bytes=64)
         side_lines = FIRST_LINES + SECOND_LINES
         third = rows.tile([P, LINES - side_lines, PACK], BF16, name="woven_third", offset=HELD_AT, align_bytes=64)
         weave_z(0, side_lines, third)
-        quantize_w2(0, 2 * P, w2_woven[:, 0 : 2 * P])
-        quantize_w2(2 * P, N, w2_woven[:, 2 * P :])
-        quantize_z(0, 0, first[:])
-        quantize_z(0, FIRST_LINES, second[:, 0:P])
-        quantize_z(0, FIRST_LINES + P, second[:, P:])
-        quantize_z(0, side_lines, third[:, 0 : P // 2])
-        quantize_z(0, side_lines + P // 2, third[:, P // 2 :])
-        quantize_w2(N, N + P, w2_side[:, 0:P])
-        quantize_w2(N + P, N + SIDE_CLASSES, w2_side[:, P:])
+        quantize_w2(0, FIRST_CLASSES, w2_woven[:])
+        quantize_w2(FIRST_CLASSES, N, w2_side[:])
+        quantize_z(0, 0, first[:, 0:P])
+        quantize_z(0, P, first[:, P:])
+        quantize_z(0, FIRST_LINES, second[:, 0 : P // 2])
+        quantize_z(0, FIRST_LINES + P // 2, second[:, P // 2 :])
+        quantize_z(0, side_lines, third[:])
 
         def second_product(target, n, b, cols, start, stop):
             nc.tensor.matmul_mx(
@@ -335,8 +336,8 @@ def tile_list_corridor_boardings_kernel(
             if u + 1 < len(runs):
                 weave_z(1, P * (u + 1), woven[u + 1])
                 if u == 0:
-                    quantize_w2(N + SIDE_CLASSES, N + 2 * P, w2_rest[:, 0 : P // 2])
-                    quantize_w2(N + 2 * P, GROUPS * N, w2_rest[:, P // 2 :])
+                    quantize_w2(N, N + P, w2_rest[:, 0:P])
+                    quantize_w2(N + P, GROUPS * N, w2_rest[:, P:])
                 quantize_z(1, P * u, woven[u][:])
                 for n in range(classes):
                     second_product(sums[u][:, P * n : P * (n + 1)], n, 1, cols, False, n == classes - 1)

@@ -82,15 +82,16 @@ def tile_list_corridor_boardings_kernel(
                 raw[:].rearrange("p a (g t w) -> p a t g w", t=PACK, w=4),
             )
 
+        load_table(0, shared.tile([P, T], I32, name="table0", offset=0))
         w4_raw = keep.tile([P, PASSES, K_PASS // 2], I32, name="w4_raw", tag="w4_raw")
         nc.sync.dma_start(w4_raw[:], w4_by_group[0])
-        lists = []
-        for name, src in (("origin", pos1), ("transfer", pos2), ("dest", pos3)):
+
+        def load_list(name, src):
             tile = keep.tile([P, LINES // 16], U16, name=name)
             nc.sync.dma_start(tile[:], src)
-            lists.append(tile)
-        origin, transfer, dest = lists
-        load_table(0, shared.tile([P, T], I32, name="table0", offset=0))
+            return tile
+
+        dest = load_list("dest", pos3)
 
         warm = keep.tile([P, 1], F32, name="warm")
         nc.vector.memset(warm[:], 0.0)
@@ -110,6 +111,9 @@ def tile_list_corridor_boardings_kernel(
 
         for x in range(4 * PASSES):
             move_rows(nc.sync, *divmod(x, 4))
+            if x == 7:
+                transfer = load_list("transfer", pos2)
+                origin = load_list("origin", pos1)
             if x in (3, 7):
                 later = 1 + x // 4
                 load_table(later, last.tile([P, T], I32, name=f"table{later}", offset=LAST_AT * (later - 1)))

@@ -22,17 +22,14 @@ K_PASS = P * PACK
 PASSES = K // K_PASS
 GROUPS = H // K_PASS
 BANK = 512
-WINDOW = 2048
 SLOTS = GROUPS * PACK
-SIDE_GAINS = (0, 1)
+HALF = LINES // 2
 FIRST_CLASSES = 256
-FIRST_LINES = 192
-SECOND_LINES = 192
-HELD_ON = {2: 0, 3: 0, 4: 3, 5: 3, 6: 5, 7: 5}
+SIDE_CLASSES = 64
 EDGE = 512
+ROW = 4 * LINES
 LAST_AT = 4 * T + PASSES * H
 W4_LATE_AT = 4 * SLOTS * N + 512
-HELD_AT = 4 * WINDOW * (SLOTS - 2)
 
 
 def tile_list_corridor_boardings_kernel(
@@ -41,9 +38,9 @@ def tile_list_corridor_boardings_kernel(
     nc = tc.nc
     with ExitStack() as ctx:
         keep = ctx.enter_context(tc.tile_pool(name="keep", bufs=1))
-        ring = ctx.enter_context(tc.tile_pool(name="ring", bufs=1))
         shared = ctx.enter_context(tc.tile_pool(name="shared", bufs=1))
         last = ctx.enter_context(tc.tile_pool(name="last", bufs=1))
+        spare = ctx.enter_context(tc.tile_pool(name="spare", bufs=1))
         rows = ctx.enter_context(tc.tile_pool(name="rows", bufs=1))
         moving = ctx.enter_context(tc.tile_pool(name="moving", bufs=1))
         psum = ctx.enter_context(tc.psum_pool(name="psum", bufs=8))
@@ -75,11 +72,13 @@ def tile_list_corridor_boardings_kernel(
         w4_by_group = w4_words.bitcast(I32).rearrange("a p (b w) -> b p a w", b=GROUPS)
         w4 = {}
 
-        def order_w4(b, raw, tile):
-            w4[b] = tile
+        def order_w4(first, count, raw, tile):
+            for x in range(count):
+                w4[first + x] = tile[:, :, 2 * P * x : 2 * P * (x + 1)]
+            lo = first % PACK
             nc.vector.tensor_copy(
-                tile[:].bitcast(I32).rearrange("p a (t g w) -> p a t g w", t=PACK, w=4),
-                raw[:].rearrange("p a (g t w) -> p a t g w", t=PACK, w=4),
+                tile[:].bitcast(I32).rearrange("p a (t g w) -> p a t g w", t=count, w=4),
+                raw[:].rearrange("p a (g t w) -> p a t g w", t=PACK, w=4)[:, :, lo : lo + count],
             )
 
         load_table(0, shared.tile([P, T], I32, name="table0", offset=0))
@@ -98,7 +97,7 @@ def tile_list_corridor_boardings_kernel(
         warm_out = keep.tile([P, 1], F32, name="warm_out")
         nc.scalar.activation(warm_out[:], warm[:], ACT.Sigmoid)
 
-        h_tiles = [rows.tile([P, WINDOW], F32, name=f"h{x}", offset=4 * WINDOW * x) for x in range(SLOTS)]
+        h_tiles = [rows.tile([P, S], F32, name=f"h{x}", offset=4 * S * x) for x in range(SLOTS)]
         picked_scales = keep.tile([P, S], U8, name="picked_scales")
         nc.vector.tensor_copy(picked_scales[:], scale_window[:].indirect(stops[:]))
         plane_tile = keep.tile([P, PASSES, S], U8, name="planes", align_bytes=64)
@@ -136,7 +135,7 @@ def tile_list_corridor_boardings_kernel(
                 nc.vector.tensor_copy(picked[a][:, lo : lo + width], table[a][:].bitcast(U32).indirect(offsets))
 
         gather(0, S, moving.tile([P, S], U32, name="picked0", offset=0 * 4 * S, align_bytes=64))
-        order_w4(0, w4_raw, keep.tile([P, PASSES, 2 * K_PASS], U8, name="w4_0", align_bytes=64))
+        order_w4(0, PACK, w4_raw, keep.tile([P, PASSES, 2 * K_PASS], U8, name="w4_0", align_bytes=64))
 
         gather(1, S, moving.tile([P, S], U32, name="picked1", offset=1 * 4 * S, align_bytes=64))
         late = shared.tile([P, SLOTS * N], F32, name="late", offset=0)
@@ -144,16 +143,20 @@ def tile_list_corridor_boardings_kernel(
         w4_late = shared.tile([P, PASSES, K_PASS // 2], I32, name="w4_late", offset=W4_LATE_AT)
         nc.sync.dma_start(w4_late[:], w4_by_group[1])
         w2_by_slot = w2.rearrange("(b g t i) n -> b t g i n", b=GROUPS, t=PACK, i=8)
-        for j in range(SLOTS):
-            nc.sync.dma_start(late[:, N * j : N * (j + 1)], w2_by_slot[j // PACK, j % PACK])
         gain_by_slot = gain.rearrange("(b g t i) -> b t g i", b=GROUPS, t=PACK, i=8)
         gains = [gain_tile[:, 8 * j : 8 * j + 1] for j in range(SLOTS)]
-        with nc.allow_non_contiguous_dma(reason="one gain to a partition"):
-            for j in range(SLOTS):
-                nc.sync.dma_start(gains[j], gain_by_slot[j // PACK, j % PACK].unsqueeze(2))
+        for b in range(GROUPS):
+            for t in range(PACK):
+                j = PACK * b + t
+                nc.sync.dma_start(late[:, N * j : N * (j + 1)], w2_by_slot[b, t])
+            with nc.allow_non_contiguous_dma(reason="one gain to a partition"):
+                for t in range(PACK):
+                    nc.sync.dma_start(gains[PACK * b + t], gain_by_slot[b, t].unsqueeze(2))
 
         gather(2, BANK, moving.tile([P, S], U32, name="picked2", offset=2 * 4 * S, align_bytes=64))
-        order_w4(1, w4_late, last.tile([P, PASSES, 2 * K_PASS], U8, name="w4_1", offset=LAST_AT, align_bytes=64))
+        for pair in range(2):
+            at = LAST_AT + 2 * ROW * pair + ROW - PASSES * 2 * P
+            order_w4(PACK + 2 * pair, 2, w4_late, last.tile([P, PASSES, 4 * P], U8, name=f"w4_late{pair}", offset=at, align_bytes=64))
 
         banks = {}
 
@@ -162,7 +165,7 @@ def tile_list_corridor_boardings_kernel(
                 banks[j, c] = psum.tile([P, BANK], F32, name="bank", tag="bank")
             nc.tensor.matmul_mx(
                 banks[j, c][:],
-                lhsT=w4[j // PACK][:, a, 2 * P * (j % PACK) : 2 * P * (j % PACK + 1)].bitcast(FP4X4),
+                lhsT=w4[j][:, a].bitcast(FP4X4),
                 lhsT_scale=w4s[:, a, P * j : P * (j + 1)],
                 rhs=picked[a][:, BANK * c : BANK * (c + 1)].bitcast(FP8X4),
                 rhs_scale=planes[a][:, BANK * c : BANK * (c + 1)],
@@ -170,70 +173,69 @@ def tile_list_corridor_boardings_kernel(
                 stop=(a == PASSES - 1),
             )
 
-        w2_codes = rows.tile([P, GROUPS, N], U32, name="w2_codes", offset=HELD_AT + 2048, align_bytes=64)
-        w2_scales = keep.tile([P, GROUPS, N], U8, name="w2_scales", align_bytes=64)
-        w2_woven = shared.tile([P, FIRST_CLASSES, PACK], BF16, name="w2_woven", offset=W4_LATE_AT, align_bytes=64)
-
-        def weave_w2(b, lo, hi, target, side):
-            by_slot = late[:, PACK * N * b : PACK * N * (b + 1)].rearrange("p (t n) -> p t n", t=PACK)
-            target = target.rearrange("p (c i) t -> p c t i", i=2)
-            source = by_slot[:, :, lo:hi].rearrange("p t (c i) -> p c t i", i=2)
-            if side:
-                nc.gpsimd.tensor_scalar(target, source, 1.0, 0.0, MULT, ADD)
+        def weave_w2(b, lo, target, engine):
+            source = late[:, PACK * N * b : PACK * N * (b + 1)].rearrange("p (t n) -> p t n", t=PACK)[:, :, lo : lo + target.shape[1]]
+            if engine is nc.gpsimd:
+                nc.gpsimd.tensor_scalar(target[:], source.rearrange("p t n -> p n t"), 1.0, 0.0, MULT, ADD)
             else:
-                nc.scalar.copy(target, source)
-
-        def quantize_w2(lo, hi, source):
-            codes = w2_codes[:].rearrange("p b n -> p (b n)")
-            scales = w2_scales[:].rearrange("p b n -> p (b n)")
-            nc.vector.quantize_mx(codes[:, lo:hi].bitcast(FP8X4), scales[:, lo:hi], source.rearrange("p n t -> p (n t)"))
+                nc.scalar.copy(target[:].rearrange("p (c i) t -> p c t i", i=2), source.rearrange("p t (c i) -> p c t i", i=2))
 
         gate = [keep.tile([P, PACK, LINES], F32, name=f"gate{b}") for b in range(GROUPS)]
         poly = [keep.tile([P, PACK, LINES], F32, name=f"poly{b}") for b in range(GROUPS)]
-        one_d = {}
+        gate_flat = [tile[:].rearrange("p t m -> p (t m)") for tile in gate]
+        one_d = {
+            0: gate[0][:, 0, :],
+            1: keep.tile([P, LINES], F32, name="one_d1")[:],
+            2: gate[0][:, 1, :],
+            3: keep.tile([P, LINES], F32, name="one_d3")[:],
+            4: gate_flat[0][:, 2 * LINES + HALF : 3 * LINES + HALF],
+            5: rows.tile([P, LINES], F32, name="one_d5", offset=4 * S * SLOTS - ROW // 2)[:],
+            6: gate_flat[1][:, HALF : HALF + LINES],
+            7: gate[1][:, 2, :],
+        }
         inner = {}
 
-        def empty_bank(j, c):
-            target = h_tiles[j][:, BANK * c : BANK * (c + 1)]
-            if (j, c) == (0, 1):
-                nc.vector.tensor_copy(target, banks[j, c][:])
-            else:
-                nc.scalar.copy(target, banks[j, c][:])
+        def empty(engine, *places):
+            for j, c in places:
+                target = h_tiles[j][:, BANK * c : BANK * (c + 1)]
+                if engine is nc.vector:
+                    nc.vector.tensor_copy(target, banks[j, c][:])
+                else:
+                    nc.scalar.copy(target, banks[j, c][:])
 
-        def pick_origin(j):
-            nc.scalar.activation(gate[j // PACK][:, j % PACK, :], h_tiles[j][:].indirect(origin[:]), ACT.Sigmoid)
+        def pick_origin(*slots):
+            for j in slots:
+                nc.scalar.activation(gate[j // PACK][:, j % PACK, :], h_tiles[j][:].indirect(origin[:]), ACT.Sigmoid)
 
-        def pick_dest(j):
-            one_d[j] = ring.tile([P, LINES], F32, name=f"one_d{j}", offset=4 * LINES * j, align_bytes=64)
-            nc.vector.tensor_scalar(one_d[j][:], h_tiles[j][:].indirect(dest[:]), 1.0, 1.0, MULT, ADD)
+        def pick_dest(*slots):
+            for j in slots:
+                nc.scalar.activation(one_d[j], h_tiles[j][:].indirect(dest[:]), ACT.Copy, bias=1.0)
 
-        parts = ((0, FIRST_LINES), (FIRST_LINES, LINES))
+        def pick_transfer(*slots):
+            for j in slots:
+                if 2 <= j < 6:
+                    inner[j] = last.tile([P, LINES], F32, name=f"inner{j}", offset=LAST_AT + ROW * (j - 2))
+                elif j == 6:
+                    inner[j] = rows.tile([P, LINES], F32, name=f"inner{j}", offset=4 * S * SLOTS)
+                elif j == 0:
+                    inner[j] = spare.tile([P, LINES], F32, name=f"inner{j}", offset=0)
+                else:
+                    inner[j] = keep.tile([P, LINES], F32, name=f"inner{j}")
+                nc.vector.tensor_tensor(inner[j][:], h_tiles[j][:].indirect(transfer[:]), one_d[j], MULT)
 
-        def pick_transfer(j):
-            if j in HELD_ON:
-                at = 4 * WINDOW * HELD_ON[j] + 4 * LINES * (j % 2)
-                inner[j] = rows.tile([P, LINES], F32, name=f"inner{j}", offset=at)
-            else:
-                inner[j] = keep.tile([P, LINES], F32, name=f"inner{j}")
-            for lo, hi in parts if j == PACK - 1 else ((0, LINES),):
-                nc.vector.tensor_tensor(inner[j][:, lo:hi], h_tiles[j][:].indirect(transfer[:, lo // 16 : hi // 16]), one_d[j][:, lo:hi], MULT)
-
-        def add_gain(j, lo=0, hi=LINES):
-            target = poly[j // PACK][:, j % PACK, lo:hi]
-            if j in SIDE_GAINS or (j, lo) == (PACK - 1, 0):
-                nc.gpsimd.tensor_scalar(target, inner[j][:, lo:hi], gains[j], gains[j], MULT, ADD)
-            else:
-                nc.scalar.activation(target, inner[j][:, lo:hi], ACT.Identity, bias=gains[j], scale=gains[j])
+        def add_gain(engine, *slots):
+            for j in slots:
+                engine.tensor_scalar(poly[j // PACK][:, j % PACK, :], inner[j][:], gains[j], gains[j], MULT, ADD)
 
         classes = N // P
         runs = [slice(lo, lo + P) for lo in range(0, LINES, P)]
         z_scales = keep.tile([P, GROUPS, LINES], U8, name="z_scales", align_bytes=64)
-        z_codes = {}
+        z_codes = [keep.tile([P, LINES], U32, name=f"z_codes{b}", align_bytes=64) for b in range(GROUPS)]
 
-        def weave_z(b, lo, tile, engine=nc.vector):
+        def weave_z(b, lo, tile):
             cols = slice(lo, lo + tile.shape[1])
-            engine.tensor_tensor(
-                tile[:].rearrange("p (c i) t -> p c t i", i=2),
+            nc.vector.tensor_tensor(
+                tile.rearrange("p (c i) t -> p c t i", i=2),
                 poly[b][:, :, cols].rearrange("p t (c i) -> p c t i", i=2),
                 gate[b][:, :, cols].rearrange("p t (c i) -> p c t i", i=2),
                 MULT,
@@ -247,72 +249,59 @@ def tile_list_corridor_boardings_kernel(
         for a in range(PASSES):
             for j, c in ahead:
                 first_product(j, c, a)
-        for j, c in ahead[:4]:
-            empty_bank(j, c)
+        empty(nc.scalar, (0, 0), (1, 0))
+        empty(nc.vector, (0, 1))
+        empty(nc.scalar, (1, 1))
         for j in range(PACK, SLOTS):
             for c in range(2):
                 for a in range(PASSES):
                     first_product(j, c, a)
-        weave_w2(0, 0, FIRST_CLASSES, w2_woven[:], True)
-
-        def empty_slot(j):
-            for c in range(2):
-                empty_bank(j, c)
-
-        def pick_pair(j):
-            for x in (j, j + 1):
-                pick_dest(x)
-            for x in (j, j + 1):
-                pick_transfer(x)
-
-        empty_slot(2)
-        empty_slot(3)
-        pick_pair(0)
-        add_gain(0)
-        add_gain(1)
-        w2_side = ring.tile([P, N - FIRST_CLASSES, PACK], BF16, name="w2_side", offset=0, align_bytes=64)
-        weave_w2(0, FIRST_CLASSES, N, w2_side[:], True)
+        w2_parts = [keep.tile([P, FIRST_CLASSES, PACK], BF16, name="w2_first", align_bytes=64)]
+        weave_w2(0, 0, w2_parts[0], nc.gpsimd)
+        empty(nc.vector, (2, 0), (2, 1), (3, 0))
+        pick_dest(0, 1, 2)
+        pick_transfer(0, 1)
+        add_gain(nc.gpsimd, 0, 1)
+        w2_parts.append(spare.tile([P, SIDE_CLASSES, PACK], BF16, name="w2_second", offset=0, align_bytes=64))
+        weave_w2(0, FIRST_CLASSES, w2_parts[1], nc.gpsimd)
         pick_origin(0)
-        pick_pair(2)
-        empty_slot(4)
+        empty(nc.vector, (3, 1), (4, 0), (4, 1))
+        pick_dest(3)
+        empty(nc.scalar, (5, 0))
+        pick_dest(4)
+        pick_transfer(2, 3)
+        add_gain(nc.gpsimd, 2, 3)
+        w2_parts.append(last.tile([P, SIDE_CLASSES, PACK], BF16, name="w2_third", offset=LAST_AT, align_bytes=64))
+        weave_w2(0, FIRST_CLASSES + SIDE_CLASSES, w2_parts[2], nc.gpsimd)
         pick_origin(1)
-        empty_slot(5)
-        pick_origin(2)
-        pick_origin(3)
-        add_gain(2, *parts[0])
-        add_gain(3, *parts[0])
-        first = keep.tile([P, FIRST_LINES, PACK], BF16, name="woven_first", align_bytes=64)
-        weave_z(0, 0, first, nc.gpsimd)
-        add_gain(2, *parts[1])
-        add_gain(3, *parts[1])
-        pick_pair(4)
-        second = ring.tile([P, SECOND_LINES, PACK], BF16, name="woven_second", offset=4 * LINES * 4, align_bytes=64)
-        weave_z(0, FIRST_LINES, second, nc.gpsimd)
-        empty_slot(6)
-        pick_origin(4)
-        empty_slot(7)
-        pick_origin(5)
-        pick_pair(6)
-        add_gain(4)
-        add_gain(5)
-        pick_origin(6)
-        pick_origin(7)
-        add_gain(6)
-        add_gain(7)
-        w2_rest = rows.tile([P, N, PACK], BF16, name="w2_rest", offset=HELD_AT + 5120, align_bytes=64)
-        weave_w2(1, 0, N, w2_rest[:], False)
-        z_codes[0] = ring.tile([P, LINES], U32, name="z_codes0", offset=4 * LINES * (SLOTS - 2), align_bytes=64)
-        z_codes[1] = keep.tile([P, LINES], U32, name="z_codes1", align_bytes=64)
-        side_lines = FIRST_LINES + SECOND_LINES
-        third = rows.tile([P, LINES - side_lines, PACK], BF16, name="woven_third", offset=HELD_AT, align_bytes=64)
-        weave_z(0, side_lines, third)
-        quantize_w2(0, FIRST_CLASSES, w2_woven[:])
-        quantize_w2(FIRST_CLASSES, N, w2_side[:])
-        quantize_z(0, 0, first[:, 0:P])
-        quantize_z(0, P, first[:, P:])
-        quantize_z(0, FIRST_LINES, second[:, 0 : P // 2])
-        quantize_z(0, FIRST_LINES + P // 2, second[:, P // 2 :])
-        quantize_z(0, side_lines, third[:])
+        empty(nc.vector, (5, 1), (6, 0), (6, 1))
+        pick_dest(5, 6)
+        pick_transfer(4, 5)
+        add_gain(nc.gpsimd, 4, 5)
+        pick_origin(2, 3)
+        empty(nc.vector, (7, 0), (7, 1))
+        pick_dest(7)
+        pick_transfer(6)
+
+        w2_codes = last.tile([P, GROUPS, N], U32, name="w2_codes", offset=LAST_AT + 2 * ROW - ROW, align_bytes=64)
+        w2_scales = keep.tile([P, GROUPS, N], U8, name="w2_scales", align_bytes=64)
+
+        def quantize_w2(b, lo, source):
+            cols = slice(lo, lo + source.shape[1])
+            nc.vector.quantize_mx(w2_codes[:, b, cols].bitcast(FP8X4), w2_scales[:, b, cols], source[:].rearrange("p n t -> p (n t)"))
+
+        for lo, part in zip((0, FIRST_CLASSES, FIRST_CLASSES + SIDE_CLASSES), w2_parts):
+            quantize_w2(0, lo, part)
+        pick_transfer(7)
+        pick_origin(7, 4, 5, 6)
+        add_gain(nc.vector, 6, 7)
+        w2_rest = rows.tile([P, N, PACK], BF16, name="w2_rest", offset=4 * S * 5, align_bytes=64)
+        weave_w2(1, 0, w2_rest, nc.scalar)
+        woven0 = last.tile([P, LINES, PACK], BF16, name="woven0", offset=LAST_AT + 3 * ROW, align_bytes=64)
+        for lo in (0, HALF):
+            weave_z(0, lo, woven0[:, lo : lo + HALF])
+        for lo in (0, HALF):
+            quantize_z(0, lo, woven0[:, lo : lo + HALF])
 
         def second_product(target, n, b, cols, start, stop):
             nc.tensor.matmul_mx(
@@ -334,20 +323,21 @@ def tile_list_corridor_boardings_kernel(
         for n in range(classes):
             second_product(last_sums[n][:, 0:P], n, 0, runs[-1], True, False)
         woven = [keep.tile([P, P, PACK], BF16, name=f"woven1{u}", align_bytes=64) for u in range(len(runs))]
-        weave_z(1, 0, woven[0])
+        for u in range(3):
+            weave_z(1, P * u, woven[u][:])
+            if u:
+                quantize_z(1, P * (u - 1), woven[u - 1][:])
+        quantize_w2(1, 0, w2_rest)
+        weave_z(1, 3 * P, woven[3][:])
+        for u in (2, 3):
+            quantize_z(1, P * u, woven[u][:])
         for u, cols in enumerate(runs):
             result = keep.tile([P, classes, P], F32, name=f"result{u}")
             if u + 1 < len(runs):
-                weave_z(1, P * (u + 1), woven[u + 1])
-                if u == 0:
-                    quantize_w2(N, N + P, w2_rest[:, 0:P])
-                    quantize_w2(N + P, GROUPS * N, w2_rest[:, P:])
-                quantize_z(1, P * u, woven[u][:])
                 for n in range(classes):
                     second_product(sums[u][:, P * n : P * (n + 1)], n, 1, cols, False, n == classes - 1)
                 nc.scalar.copy(result[:].rearrange("p n m -> p (n m)"), sums[u][:, 0 : classes * P])
             else:
-                quantize_z(1, P * u, woven[u][:])
                 for n in range(classes):
                     second_product(last_sums[n][:, 0:P], n, 1, cols, False, True)
                     if n == 1:

@@ -56,18 +56,19 @@ def tile_list_corridor_boardings_kernel(
         for lo, hi in ((0, 48), (64, 96)):
             nc.vector.memset(scale_window[lo:hi, :].bitcast(I32), 0)
 
-        w4s_raw = keep.tile([P, PASSES, H // 4], I32, name="w4s_raw")
-        for q in range(4):
-            nc.sync.dma_start(
-                w4s_raw[32 * q : 32 * q + 4],
-                w4_scales[:, 4 * q : 4 * q + 4, :].bitcast(I32).rearrange("a r w -> r a w"),
-            )
+        def load_w4_scales(b, raw):
+            for q in range(4):
+                rows_of_q = w4_scales[:, 4 * q : 4 * q + 4, K_PASS * b : K_PASS * (b + 1)]
+                nc.sync.dma_start(raw[32 * q : 32 * q + 4], rows_of_q.bitcast(I32).rearrange("a r w -> r a w"))
+
+        w4s_raw = keep.tile([P, PASSES, K_PASS // 4], I32, name="w4s_raw")
+        load_w4_scales(0, w4s_raw)
 
         table = {}
 
-        def load_table(a, tile):
+        def load_table(a, tile, lo=0, hi=T):
             table[a] = tile
-            nc.sync.dma_start(tile[:], tab_words[a].rearrange("p t i -> p (t i)").bitcast(I32))
+            nc.sync.dma_start(tile[:, lo:hi], tab_words[a].rearrange("p t i -> p (t i)").bitcast(I32)[:, lo:hi])
 
         w4_by_group = w4_words.bitcast(I32).rearrange("a p (b w) -> b p a w", b=GROUPS)
         w4 = {}
@@ -91,6 +92,7 @@ def tile_list_corridor_boardings_kernel(
             return tile
 
         dest = load_list("dest", pos3)
+        load_table(1, last.tile([P, T], I32, name="table1", offset=0), 0, T // 2)
 
         warm = keep.tile([P, 1], F32, name="warm")
         nc.vector.memset(warm[:], 0.0)
@@ -113,18 +115,27 @@ def tile_list_corridor_boardings_kernel(
             if x == 7:
                 transfer = load_list("transfer", pos2)
                 origin = load_list("origin", pos1)
-            if x in (3, 7):
-                later = 1 + x // 4
-                load_table(later, last.tile([P, T], I32, name=f"table{later}", offset=LAST_AT * (later - 1)))
+            if x == 3:
+                load_table(1, table[1], T // 2, T)
+            if x == 7:
+                load_table(2, last.tile([P, T], I32, name="table2", offset=LAST_AT))
 
-        w4s = last.tile([P, PASSES, H], U8, name="w4s", offset=4 * T, align_bytes=64)
-        nc.vector.memset(w4s[:].bitcast(I32), 0)
+        def order_w4_scales(engine, target, raw):
+            engine.tensor_copy(
+                target.bitcast(I32).rearrange("p a (t g w) -> p a t g w", t=PACK, w=2),
+                raw.rearrange("p a (g t w) -> p a t g w", t=PACK, w=2),
+            )
+
+        w4s = [
+            last.tile([P, PASSES, K_PASS], U8, name="w4s0", offset=4 * T, align_bytes=64),
+            keep.tile([P, PASSES, K_PASS], U8, name="w4s1", align_bytes=64),
+        ]
+        w4s_late = last.tile([P, PASSES, K_PASS // 4], I32, name="w4s_late", offset=4 * T + PASSES * K_PASS)
+        nc.vector.memset(w4s[0][:].bitcast(I32), 0)
+        nc.vector.memset(w4s_late[:], 0)
         for q in range(4):
             live = slice(32 * q, 32 * q + 4)
-            nc.vector.tensor_copy(
-                w4s[live].bitcast(I32).rearrange("p a (b t g w) -> p (a b) t g w", b=GROUPS, t=PACK, w=2),
-                w4s_raw[live].rearrange("p a (b g t w) -> p (a b) t g w", b=GROUPS, t=PACK, w=2),
-            )
+            order_w4_scales(nc.vector, w4s[0][live], w4s_raw[live])
 
         picked = {}
 
@@ -149,6 +160,8 @@ def tile_list_corridor_boardings_kernel(
             for t in range(PACK):
                 j = PACK * b + t
                 nc.sync.dma_start(late[:, N * j : N * (j + 1)], w2_by_slot[b, t])
+            if b == 0:
+                load_w4_scales(1, w4s_late)
             with nc.allow_non_contiguous_dma(reason="one gain to a partition"):
                 for t in range(PACK):
                     nc.sync.dma_start(gains[PACK * b + t], gain_by_slot[b, t].unsqueeze(2))
@@ -166,7 +179,7 @@ def tile_list_corridor_boardings_kernel(
             nc.tensor.matmul_mx(
                 banks[j, c][:],
                 lhsT=w4[j][:, a].bitcast(FP4X4),
-                lhsT_scale=w4s[:, a, P * j : P * (j + 1)],
+                lhsT_scale=w4s[j // PACK][:, a, P * (j % PACK) : P * (j % PACK + 1)],
                 rhs=picked[a][:, BANK * c : BANK * (c + 1)].bitcast(FP8X4),
                 rhs_scale=planes[a][:, BANK * c : BANK * (c + 1)],
                 start=(a == 0),
@@ -252,6 +265,7 @@ def tile_list_corridor_boardings_kernel(
         empty(nc.scalar, (0, 0), (1, 0))
         empty(nc.vector, (0, 1))
         empty(nc.scalar, (1, 1))
+        order_w4_scales(nc.gpsimd, w4s[1][:], w4s_late[:])
         for j in range(PACK, SLOTS):
             for c in range(2):
                 for a in range(PASSES):

@@ -24,8 +24,6 @@ GROUPS = H // K_PASS
 BANK = 512
 SLOTS = GROUPS * PACK
 HALF = LINES // 2
-FIRST_CLASSES = 256
-SIDE_CLASSES = 64
 EDGE = 512
 ROW = 4 * LINES
 LAST_AT = 4 * T + PASSES * H
@@ -40,7 +38,6 @@ def tile_list_corridor_boardings_kernel(
         keep = ctx.enter_context(tc.tile_pool(name="keep", bufs=1))
         shared = ctx.enter_context(tc.tile_pool(name="shared", bufs=1))
         last = ctx.enter_context(tc.tile_pool(name="last", bufs=1))
-        spare = ctx.enter_context(tc.tile_pool(name="spare", bufs=1))
         rows = ctx.enter_context(tc.tile_pool(name="rows", bufs=1))
         moving = ctx.enter_context(tc.tile_pool(name="moving", bufs=1))
         psum = ctx.enter_context(tc.psum_pool(name="psum", bufs=8))
@@ -56,13 +53,11 @@ def tile_list_corridor_boardings_kernel(
         for lo, hi in ((0, 48), (64, 96)):
             nc.vector.memset(scale_window[lo:hi, :].bitcast(I32), 0)
 
-        def load_w4_scales(b, raw):
+        w4s_raw = [keep.tile([P, PASSES, K_PASS // 4], I32, name=f"w4s_raw{b}") for b in range(GROUPS)]
+        for b, queue in enumerate((nc.sync, nc.gpsimd)):
             for q in range(4):
                 rows_of_q = w4_scales[:, 4 * q : 4 * q + 4, K_PASS * b : K_PASS * (b + 1)]
-                nc.sync.dma_start(raw[32 * q : 32 * q + 4], rows_of_q.bitcast(I32).rearrange("a r w -> r a w"))
-
-        w4s_raw = keep.tile([P, PASSES, K_PASS // 4], I32, name="w4s_raw")
-        load_w4_scales(0, w4s_raw)
+                queue.dma_start(w4s_raw[b][32 * q : 32 * q + 4], rows_of_q.bitcast(I32).rearrange("a r w -> r a w"))
 
         table = {}
 
@@ -120,22 +115,19 @@ def tile_list_corridor_boardings_kernel(
             if x == 7:
                 load_table(2, last.tile([P, T], I32, name="table2", offset=LAST_AT))
 
-        def order_w4_scales(engine, target, raw):
-            engine.tensor_copy(
-                target.bitcast(I32).rearrange("p a (t g w) -> p a t g w", t=PACK, w=2),
-                raw.rearrange("p a (g t w) -> p a t g w", t=PACK, w=2),
-            )
+        w4s = []
 
-        w4s = [
-            last.tile([P, PASSES, K_PASS], U8, name="w4s0", offset=4 * T, align_bytes=64),
-            keep.tile([P, PASSES, K_PASS], U8, name="w4s1", align_bytes=64),
-        ]
-        w4s_late = last.tile([P, PASSES, K_PASS // 4], I32, name="w4s_late", offset=4 * T + PASSES * K_PASS)
-        nc.vector.memset(w4s[0][:].bitcast(I32), 0)
-        nc.vector.memset(w4s_late[:], 0)
-        for q in range(4):
-            live = slice(32 * q, 32 * q + 4)
-            order_w4_scales(nc.vector, w4s[0][live], w4s_raw[live])
+        def order_w4_scales(b, pool, at):
+            w4s.append(pool.tile([P, PASSES, K_PASS], U8, name=f"w4s{b}", offset=at, align_bytes=64))
+            nc.vector.memset(w4s[b][:].bitcast(I32), 0)
+            for q in range(4):
+                live = slice(32 * q, 32 * q + 4)
+                nc.vector.tensor_copy(
+                    w4s[b][live].bitcast(I32).rearrange("p a (t g w) -> p a t g w", t=PACK, w=2),
+                    w4s_raw[b][live].rearrange("p a (g t w) -> p a t g w", t=PACK, w=2),
+                )
+
+        order_w4_scales(0, last, 4 * T)
 
         picked = {}
 
@@ -147,6 +139,8 @@ def tile_list_corridor_boardings_kernel(
 
         gather(0, S, moving.tile([P, S], U32, name="picked0", offset=0 * 4 * S, align_bytes=64))
         order_w4(0, PACK, w4_raw, keep.tile([P, PASSES, 2 * K_PASS], U8, name="w4_0", align_bytes=64))
+
+        order_w4_scales(1, shared, 4 * T - EDGE)
 
         gather(1, S, moving.tile([P, S], U32, name="picked1", offset=1 * 4 * S, align_bytes=64))
         late = shared.tile([P, SLOTS * N], F32, name="late", offset=0)
@@ -160,8 +154,6 @@ def tile_list_corridor_boardings_kernel(
             for t in range(PACK):
                 j = PACK * b + t
                 nc.sync.dma_start(late[:, N * j : N * (j + 1)], w2_by_slot[b, t])
-            if b == 0:
-                load_w4_scales(1, w4s_late)
             with nc.allow_non_contiguous_dma(reason="one gain to a partition"):
                 for t in range(PACK):
                     nc.sync.dma_start(gains[PACK * b + t], gain_by_slot[b, t].unsqueeze(2))
@@ -186,8 +178,8 @@ def tile_list_corridor_boardings_kernel(
                 stop=(a == PASSES - 1),
             )
 
-        def weave_w2(b, lo, target, engine):
-            source = late[:, PACK * N * b : PACK * N * (b + 1)].rearrange("p (t n) -> p t n", t=PACK)[:, :, lo : lo + target.shape[1]]
+        def weave_w2(b, target, engine):
+            source = late[:, PACK * N * b : PACK * N * (b + 1)].rearrange("p (t n) -> p t n", t=PACK)
             if engine is nc.gpsimd:
                 nc.gpsimd.tensor_scalar(target[:], source.rearrange("p t n -> p n t"), 1.0, 0.0, MULT, ADD)
             else:
@@ -230,8 +222,6 @@ def tile_list_corridor_boardings_kernel(
                     inner[j] = last.tile([P, LINES], F32, name=f"inner{j}", offset=LAST_AT + ROW * (j - 2))
                 elif j == 6:
                     inner[j] = rows.tile([P, LINES], F32, name=f"inner{j}", offset=4 * S * SLOTS)
-                elif j == 0:
-                    inner[j] = spare.tile([P, LINES], F32, name=f"inner{j}", offset=0)
                 else:
                     inner[j] = keep.tile([P, LINES], F32, name=f"inner{j}")
                 nc.vector.tensor_tensor(inner[j][:], h_tiles[j][:].indirect(transfer[:]), one_d[j], MULT)
@@ -258,26 +248,21 @@ def tile_list_corridor_boardings_kernel(
             cols = slice(lo, lo + source.shape[1])
             nc.vector.quantize_mx(z_codes[b][:, cols].bitcast(FP8X4), z_scales[:, b, cols], source.rearrange("p m t -> p (m t)"))
 
-        ahead = [(0, 0), (1, 0), (0, 1), (1, 1), (2, 0), (2, 1), (3, 0), (3, 1)]
+        ahead = [(j, c) for c in range(2) for j in range(3)] + [(3, 0), (3, 1)]
         for a in range(PASSES):
             for j, c in ahead:
                 first_product(j, c, a)
-        empty(nc.scalar, (0, 0), (1, 0))
-        empty(nc.vector, (0, 1))
-        empty(nc.scalar, (1, 1))
-        order_w4_scales(nc.gpsimd, w4s[1][:], w4s_late[:])
+        empty(nc.scalar, (0, 0), (1, 0), (0, 1))
+        empty(nc.vector, (2, 0), (1, 1), (2, 1), (3, 0))
         for j in range(PACK, SLOTS):
             for c in range(2):
                 for a in range(PASSES):
                     first_product(j, c, a)
-        w2_parts = [keep.tile([P, FIRST_CLASSES, PACK], BF16, name="w2_first", align_bytes=64)]
-        weave_w2(0, 0, w2_parts[0], nc.gpsimd)
-        empty(nc.vector, (2, 0), (2, 1), (3, 0))
+        w2_first = keep.tile([P, N, PACK], BF16, name="w2_first", align_bytes=64)
+        weave_w2(0, w2_first, nc.gpsimd)
         pick_dest(0, 1, 2)
         pick_transfer(0, 1)
         add_gain(nc.gpsimd, 0, 1)
-        w2_parts.append(spare.tile([P, SIDE_CLASSES, PACK], BF16, name="w2_second", offset=0, align_bytes=64))
-        weave_w2(0, FIRST_CLASSES, w2_parts[1], nc.gpsimd)
         pick_origin(0)
         empty(nc.vector, (3, 1), (4, 0), (4, 1))
         pick_dest(3)
@@ -285,13 +270,11 @@ def tile_list_corridor_boardings_kernel(
         pick_dest(4)
         pick_transfer(2, 3)
         add_gain(nc.gpsimd, 2, 3)
-        w2_parts.append(last.tile([P, SIDE_CLASSES, PACK], BF16, name="w2_third", offset=LAST_AT, align_bytes=64))
-        weave_w2(0, FIRST_CLASSES + SIDE_CLASSES, w2_parts[2], nc.gpsimd)
         pick_origin(1)
         empty(nc.vector, (5, 1), (6, 0), (6, 1))
         pick_dest(5, 6)
         pick_transfer(4, 5)
-        add_gain(nc.gpsimd, 4, 5)
+        add_gain(nc.gpsimd, 4)
         pick_origin(2, 3)
         empty(nc.vector, (7, 0), (7, 1))
         pick_dest(7)
@@ -304,13 +287,12 @@ def tile_list_corridor_boardings_kernel(
             cols = slice(lo, lo + source.shape[1])
             nc.vector.quantize_mx(w2_codes[:, b, cols].bitcast(FP8X4), w2_scales[:, b, cols], source[:].rearrange("p n t -> p (n t)"))
 
-        for lo, part in zip((0, FIRST_CLASSES, FIRST_CLASSES + SIDE_CLASSES), w2_parts):
-            quantize_w2(0, lo, part)
+        quantize_w2(0, 0, w2_first)
         pick_transfer(7)
         pick_origin(7, 4, 5, 6)
-        add_gain(nc.vector, 6, 7)
+        add_gain(nc.vector, 5, 6, 7)
         w2_rest = rows.tile([P, N, PACK], BF16, name="w2_rest", offset=4 * S * 5, align_bytes=64)
-        weave_w2(1, 0, w2_rest, nc.scalar)
+        weave_w2(1, w2_rest, nc.scalar)
         woven0 = last.tile([P, LINES, PACK], BF16, name="woven0", offset=LAST_AT + 3 * ROW, align_bytes=64)
         for lo in (0, HALF):
             weave_z(0, lo, woven0[:, lo : lo + HALF])

@@ -25,6 +25,7 @@ BANK = 512
 SLOTS = GROUPS * PACK
 HALF = LINES // 2
 EDGE = 512
+EARLY = LINES - P
 ROW = 4 * LINES
 LAST_AT = 4 * T + PASSES * H
 W4_LATE_AT = 4 * SLOTS * N + 512
@@ -39,6 +40,7 @@ def tile_list_corridor_boardings_kernel(
         shared = ctx.enter_context(tc.tile_pool(name="shared", bufs=1))
         last = ctx.enter_context(tc.tile_pool(name="last", bufs=1))
         rows = ctx.enter_context(tc.tile_pool(name="rows", bufs=1))
+        ending = ctx.enter_context(tc.tile_pool(name="ending", bufs=1))
         moving = ctx.enter_context(tc.tile_pool(name="moving", bufs=1))
         psum = ctx.enter_context(tc.psum_pool(name="psum", bufs=8))
 
@@ -185,7 +187,10 @@ def tile_list_corridor_boardings_kernel(
             else:
                 nc.scalar.copy(target[:].rearrange("p (c i) t -> p c t i", i=2), source.rearrange("p t (c i) -> p c t i", i=2))
 
-        gate = [keep.tile([P, PACK, LINES], F32, name=f"gate{b}") for b in range(GROUPS)]
+        gate = [
+            keep.tile([P, PACK, LINES], F32, name="gate0"),
+            ending.tile([P, PACK, LINES], F32, name="gate1", offset=2 * PACK * N),
+        ]
         poly = [keep.tile([P, PACK, LINES], F32, name=f"poly{b}") for b in range(GROUPS)]
         gate_flat = [tile[:].rearrange("p t m -> p (t m)") for tile in gate]
         one_d = {
@@ -195,8 +200,8 @@ def tile_list_corridor_boardings_kernel(
             3: keep.tile([P, LINES], F32, name="one_d3")[:],
             4: gate_flat[0][:, 2 * LINES + HALF : 3 * LINES + HALF],
             5: rows.tile([P, LINES], F32, name="one_d5", offset=4 * S * SLOTS - ROW // 2)[:],
-            6: gate_flat[1][:, HALF : HALF + LINES],
-            7: gate[1][:, 2, :],
+            6: ending.tile([P, LINES], F32, name="one_d6", offset=2 * PACK * N - ROW // 2)[:],
+            7: keep.tile([P, LINES], F32, name="one_d7")[:],
         }
         inner = {}
 
@@ -208,9 +213,10 @@ def tile_list_corridor_boardings_kernel(
                 else:
                     nc.scalar.copy(target, banks[j, c][:])
 
-        def pick_origin(*slots):
+        def pick_origin(*slots, lo=0, hi=LINES):
             for j in slots:
-                nc.scalar.activation(gate[j // PACK][:, j % PACK, :], h_tiles[j][:].indirect(origin[:]), ACT.Sigmoid)
+                picked_rows = h_tiles[j][:].indirect(origin[:, lo // 16 : hi // 16])
+                nc.scalar.activation(gate[j // PACK][:, j % PACK, lo:hi], picked_rows, ACT.Sigmoid)
 
         def pick_dest(*slots):
             for j in slots:
@@ -289,15 +295,17 @@ def tile_list_corridor_boardings_kernel(
 
         quantize_w2(0, 0, w2_first)
         pick_transfer(7)
-        pick_origin(7, 4, 5, 6)
-        add_gain(nc.vector, 5, 6, 7)
-        w2_rest = rows.tile([P, N, PACK], BF16, name="w2_rest", offset=4 * S * 5, align_bytes=64)
+        w2_rest = ending.tile([P, N, PACK], BF16, name="w2_rest", offset=0, align_bytes=64)
         weave_w2(1, w2_rest, nc.scalar)
+        pick_origin(4, 5, 6, 7, hi=EARLY)
+        pick_origin(4, 5, 6, 7, lo=EARLY)
+        add_gain(nc.vector, 5, 6, 7)
         woven0 = last.tile([P, LINES, PACK], BF16, name="woven0", offset=LAST_AT + 3 * ROW, align_bytes=64)
         for lo in (0, HALF):
             weave_z(0, lo, woven0[:, lo : lo + HALF])
-        for lo in (0, HALF):
-            quantize_z(0, lo, woven0[:, lo : lo + HALF])
+        quantize_z(0, 0, woven0[:, 0:HALF])
+        quantize_w2(1, 0, w2_rest)
+        quantize_z(0, HALF, woven0[:, HALF:LINES])
 
         def second_product(target, n, b, cols, start, stop):
             nc.tensor.matmul_mx(
@@ -319,14 +327,11 @@ def tile_list_corridor_boardings_kernel(
         for n in range(classes):
             second_product(last_sums[n][:, 0:P], n, 0, runs[-1], True, False)
         woven = [keep.tile([P, P, PACK], BF16, name=f"woven1{u}", align_bytes=64) for u in range(len(runs))]
-        for u in range(3):
+        for u in range(len(runs)):
             weave_z(1, P * u, woven[u][:])
             if u:
                 quantize_z(1, P * (u - 1), woven[u - 1][:])
-        quantize_w2(1, 0, w2_rest)
-        weave_z(1, 3 * P, woven[3][:])
-        for u in (2, 3):
-            quantize_z(1, P * u, woven[u][:])
+        quantize_z(1, EARLY, woven[-1][:])
         for u, cols in enumerate(runs):
             result = keep.tile([P, classes, P], F32, name=f"result{u}")
             if u + 1 < len(runs):
@@ -336,7 +341,7 @@ def tile_list_corridor_boardings_kernel(
             else:
                 for n in range(classes):
                     second_product(last_sums[n][:, 0:P], n, 1, cols, False, True)
-                    if n == 1:
+                    if n < 2:
                         nc.vector.tensor_copy(result[:, n, :], last_sums[n][:, 0:P])
                     else:
                         nc.scalar.copy(result[:, n, :], last_sums[n][:, 0:P])

@@ -297,8 +297,8 @@ def tile_list_corridor_boardings_kernel(
         pick_transfer(7)
         w2_rest = ending.tile([P, N, PACK], BF16, name="w2_rest", offset=0, align_bytes=64)
         weave_w2(1, w2_rest, nc.scalar)
-        pick_origin(4, 5, 6, 7, hi=EARLY)
-        pick_origin(4, 5, 6, 7, lo=EARLY)
+        for lo, hi in ((0, HALF), (HALF, EARLY), (EARLY, LINES)):
+            pick_origin(4, 5, 6, 7, lo=lo, hi=hi)
         add_gain(nc.vector, 5, 6, 7)
         woven0 = last.tile([P, LINES, PACK], BF16, name="woven0", offset=LAST_AT + 3 * ROW, align_bytes=64)
         for lo in (0, HALF):

from contextlib import ExitStack

import concourse.mybir as mybir

K, T, S, LINES, H, N = 1536, 4096, 1024, 512, 1024, 384
FLOPS = 2 * K * H * S + 2 * H * N * LINES

F32 = mybir.dt.float32
BF16 = mybir.dt.bfloat16
I32 = mybir.dt.int32
U32 = mybir.dt.uint32
U16 = mybir.dt.uint16
U8 = mybir.dt.uint8
FP8X4 = mybir.dt.float8_e4m3fn_x4
FP4X4 = mybir.dt.float4_e2m1fn_x4
ACT = mybir.ActivationFunctionType
MULT, ADD = mybir.AluOpType.mult, mybir.AluOpType.add

P = 128
PACK = 4
K_PASS = P * PACK
PASSES = K // K_PASS
GROUPS = H // K_PASS
BANK = 512
SLOTS = GROUPS * PACK
HALF = LINES // 2
EDGE = 512
EARLY = LINES - P
ROW = 4 * LINES
LAST_AT = 4 * T + PASSES * H
W4_LATE_AT = 4 * SLOTS * N + 512


def tile_list_corridor_boardings_kernel(
    tc, tab_words, tab_scales, offs, w4_words, w4_scales, pos1, pos2, pos3, gain, w2, out
):
    nc = tc.nc
    with ExitStack() as ctx:
        keep = ctx.enter_context(tc.tile_pool(name="keep", bufs=1))
        shared = ctx.enter_context(tc.tile_pool(name="shared", bufs=1))
        last = ctx.enter_context(tc.tile_pool(name="last", bufs=1))
        rows = ctx.enter_context(tc.tile_pool(name="rows", bufs=1))
        ending = ctx.enter_context(tc.tile_pool(name="ending", bufs=1))
        moving = ctx.enter_context(tc.tile_pool(name="moving", bufs=1))
        psum = ctx.enter_context(tc.psum_pool(name="psum", bufs=8))

        stops = keep.tile([P, S // 16], U16, name="stops")
        nc.sync.dma_start(stops[:], offs)

        scale_window = last.tile([P, T], U8, name="scale_window", offset=4 * T - EDGE)
        scale_rows = tab_scales.bitcast(I32).rearrange("a q w -> (a q) w")
        row_base = (96, 112, 48)
        nc.sync.dma_start(scale_window[96:P, :].bitcast(I32), scale_rows[0:32])
        nc.sync.dma_start(scale_window[48:64, :].bitcast(I32), scale_rows[32:48])
        for lo, hi in ((0, 48), (64, 96)):
            nc.vector.memset(scale_window[lo:hi, :].bitcast(I32), 0)

        w4s_raw = [keep.tile([P, PASSES, K_PASS // 4], I32, name=f"w4s_raw{b}") for b in range(GROUPS)]
        for b, queue in enumerate((nc.sync, nc.gpsimd)):
            for q in range(4):
                rows_of_q = w4_scales[:, 4 * q : 4 * q + 4, K_PASS * b : K_PASS * (b + 1)]
                queue.dma_start(w4s_raw[b][32 * q : 32 * q + 4], rows_of_q.bitcast(I32).rearrange("a r w -> r a w"))

        table = {}

        def load_table(a, tile, lo=0, hi=T):
            table[a] = tile
            nc.sync.dma_start(tile[:, lo:hi], tab_words[a].rearrange("p t i -> p (t i)").bitcast(I32)[:, lo:hi])

        w4_by_group = w4_words.bitcast(I32).rearrange("a p (b w) -> b p a w", b=GROUPS)
        w4 = {}

        def order_w4(first, count, raw, tile):
            for x in range(count):
                w4[first + x] = tile[:, :, 2 * P * x : 2 * P * (x + 1)]
            lo = first % PACK
            nc.vector.tensor_copy(
                tile[:].bitcast(I32).rearrange("p a (t g w) -> p a t g w", t=count, w=4),
                raw[:].rearrange("p a (g t w) -> p a t g w", t=PACK, w=4)[:, :, lo : lo + count],
            )

        load_table(0, shared.tile([P, T], I32, name="table0", offset=0))
        w4_raw = keep.tile([P, PASSES, K_PASS // 2], I32, name="w4_raw", tag="w4_raw")
        nc.sync.dma_start(w4_raw[:], w4_by_group[0])

        def load_list(name, src):
            tile = keep.tile([P, LINES // 16], U16, name=name)
            nc.sync.dma_start(tile[:], src)
            return tile

        dest = load_list("dest", pos3)
        load_table(1, last.tile([P, T], I32, name="table1", offset=0), 0, T // 2)

        warm = keep.tile([P, 1], F32, name="warm")
        nc.vector.memset(warm[:], 0.0)
        warm_out = keep.tile([P, 1], F32, name="warm_out")
        nc.scalar.activation(warm_out[:], warm[:], ACT.Sigmoid)

        h_tiles = [rows.tile([P, S], F32, name=f"h{x}", offset=4 * S * x) for x in range(SLOTS)]
        picked_scales = keep.tile([P, S], U8, name="picked_scales")
        nc.vector.tensor_copy(picked_scales[:], scale_window[:].indirect(stops[:]))
        plane_tile = keep.tile([P, PASSES, S], U8, name="planes", align_bytes=64)
        nc.vector.memset(plane_tile[:].bitcast(I32), 0)
        planes = [plane_tile[:, a] for a in range(PASSES)]

        def move_rows(queue, a, q):
            first = row_base[a] + 4 * q
            queue.dma_start(planes[a][32 * q : 32 * q + 4, :].bitcast(I32), picked_scales[first : first + 4, :].bitcast(I32))

        for x in range(4 * PASSES):
            move_rows(nc.sync, *divmod(x, 4))
            if x == 7:
                transfer = load_list("transfer", pos2)
                origin = load_list("origin", pos1)
            if x == 3:
                load_table(1, table[1], T // 2, T)
            if x == 7:
                load_table(2, last.tile([P, T], I32, name="table2", offset=LAST_AT))

        w4s = []

        def order_w4_scales(b, pool, at):
            w4s.append(pool.tile([P, PASSES, K_PASS], U8, name=f"w4s{b}", offset=at, align_bytes=64))
            nc.vector.memset(w4s[b][:].bitcast(I32), 0)
            for q in range(4):
                live = slice(32 * q, 32 * q + 4)
                nc.vector.tensor_copy(
                    w4s[b][live].bitcast(I32).rearrange("p a (t g w) -> p a t g w", t=PACK, w=2),
                    w4s_raw[b][live].rearrange("p a (g t w) -> p a t g w", t=PACK, w=2),
                )

        order_w4_scales(0, last, 4 * T)

        picked = {}

        def gather(a, width, tile):
            picked[a] = tile
            for lo in range(0, S, width):
                offsets = stops[:, lo // 16 : (lo + width) // 16]
                nc.vector.tensor_copy(picked[a][:, lo : lo + width], table[a][:].bitcast(U32).indirect(offsets))

        gather(0, S, moving.tile([P, S], U32, name="picked0", offset=0 * 4 * S, align_bytes=64))
        order_w4(0, PACK, w4_raw, keep.tile([P, PASSES, 2 * K_PASS], U8, name="w4_0", align_bytes=64))

        order_w4_scales(1, shared, 4 * T - EDGE)

        gather(1, S, moving.tile([P, S], U32, name="picked1", offset=1 * 4 * S, align_bytes=64))
        late = shared.tile([P, SLOTS * N], F32, name="late", offset=0)
        gain_tile = shared.tile([P, SLOTS * 8], F32, name="gain_tile", offset=4 * SLOTS * N)
        w4_late = shared.tile([P, PASSES, K_PASS // 2], I32, name="w4_late", offset=W4_LATE_AT)
        nc.sync.dma_start(w4_late[:], w4_by_group[1])
        w2_by_slot = w2.rearrange("(b g t i) n -> b t g i n", b=GROUPS, t=PACK, i=8)
        gain_by_slot = gain.rearrange("(b g t i) -> b t g i", b=GROUPS, t=PACK, i=8)
        gains = [gain_tile[:, 8 * j : 8 * j + 1] for j in range(SLOTS)]
        for b in range(GROUPS):
            for t in range(PACK):
                j = PACK * b + t
                nc.sync.dma_start(late[:, N * j : N * (j + 1)], w2_by_slot[b, t])
            with nc.allow_non_contiguous_dma(reason="one gain to a partition"):
                for t in range(PACK):
                    nc.sync.dma_start(gains[PACK * b + t], gain_by_slot[b, t].unsqueeze(2))

        gather(2, BANK, moving.tile([P, S], U32, name="picked2", offset=2 * 4 * S, align_bytes=64))
        for pair in range(2):
            at = LAST_AT + 2 * ROW * pair + ROW - PASSES * 2 * P
            order_w4(PACK + 2 * pair, 2, w4_late, last.tile([P, PASSES, 4 * P], U8, name=f"w4_late{pair}", offset=at, align_bytes=64))

        banks = {}

        def first_product(j, c, a):
            if a == 0:
                banks[j, c] = psum.tile([P, BANK], F32, name="bank", tag="bank")
            nc.tensor.matmul_mx(
                banks[j, c][:],
                lhsT=w4[j][:, a].bitcast(FP4X4),
                lhsT_scale=w4s[j // PACK][:, a, P * (j % PACK) : P * (j % PACK + 1)],
                rhs=picked[a][:, BANK * c : BANK * (c + 1)].bitcast(FP8X4),
                rhs_scale=planes[a][:, BANK * c : BANK * (c + 1)],
                start=(a == 0),
                stop=(a == PASSES - 1),
            )

        def weave_w2(b, target, engine):
            source = late[:, PACK * N * b : PACK * N * (b + 1)].rearrange("p (t n) -> p t n", t=PACK)
            if engine is nc.gpsimd:
                nc.gpsimd.tensor_scalar(target[:], source.rearrange("p t n -> p n t"), 1.0, 0.0, MULT, ADD)
            else:
                nc.scalar.copy(target[:].rearrange("p (c i) t -> p c t i", i=2), source.rearrange("p t (c i) -> p c t i", i=2))

        gate = [
            keep.tile([P, PACK, LINES], F32, name="gate0"),
            ending.tile([P, PACK, LINES], F32, name="gate1", offset=2 * PACK * N),
        ]
        poly = [keep.tile([P, PACK, LINES], F32, name=f"poly{b}") for b in range(GROUPS)]
        gate_flat = [tile[:].rearrange("p t m -> p (t m)") for tile in gate]
        one_d = {
            0: gate[0][:, 0, :],
            1: keep.tile([P, LINES], F32, name="one_d1")[:],
            2: gate[0][:, 1, :],
            3: keep.tile([P, LINES], F32, name="one_d3")[:],
            4: gate_flat[0][:, 2 * LINES + HALF : 3 * LINES + HALF],
            5: rows.tile([P, LINES], F32, name="one_d5", offset=4 * S * SLOTS - ROW // 2)[:],
            6: ending.tile([P, LINES], F32, name="one_d6", offset=2 * PACK * N - ROW // 2)[:],
            7: keep.tile([P, LINES], F32, name="one_d7")[:],
        }
        inner = {}

        def empty(engine, *places):
            for j, c in places:
                target = h_tiles[j][:, BANK * c : BANK * (c + 1)]
                if engine is nc.vector:
                    nc.vector.tensor_copy(target, banks[j, c][:])
                else:
                    nc.scalar.copy(target, banks[j, c][:])

        def pick_origin(*slots, lo=0, hi=LINES):
            for j in slots:
                picked_rows = h_tiles[j][:].indirect(origin[:, lo // 16 : hi // 16])
                nc.scalar.activation(gate[j // PACK][:, j % PACK, lo:hi], picked_rows, ACT.Sigmoid)

        def pick_dest(*slots):
            for j in slots:
                nc.scalar.activation(one_d[j], h_tiles[j][:].indirect(dest[:]), ACT.Copy, bias=1.0)

        def pick_transfer(*slots):
            for j in slots:
                if 2 <= j < 6:
                    inner[j] = last.tile([P, LINES], F32, name=f"inner{j}", offset=LAST_AT + ROW * (j - 2))
                elif j == 6:
                    inner[j] = rows.tile([P, LINES], F32, name=f"inner{j}", offset=4 * S * SLOTS)
                else:
                    inner[j] = keep.tile([P, LINES], F32, name=f"inner{j}")
                nc.vector.tensor_tensor(inner[j][:], h_tiles[j][:].indirect(transfer[:]), one_d[j], MULT)

        def add_gain(engine, *slots):
            for j in slots:
                engine.tensor_scalar(poly[j // PACK][:, j % PACK, :], inner[j][:], gains[j], gains[j], MULT, ADD)

        classes = N // P
        runs = [slice(lo, lo + P) for lo in range(0, LINES, P)]
        z_scales = keep.tile([P, GROUPS, LINES], U8, name="z_scales", align_bytes=64)
        z_codes = [keep.tile([P, LINES], U32, name=f"z_codes{b}", align_bytes=64) for b in range(GROUPS)]

        def weave_z(b, lo, tile):
            cols = slice(lo, lo + tile.shape[1])
            nc.vector.tensor_tensor(
                tile.rearrange("p (c i) t -> p c t i", i=2),
                poly[b][:, :, cols].rearrange("p t (c i) -> p c t i", i=2),
                gate[b][:, :, cols].rearrange("p t (c i) -> p c t i", i=2),
                MULT,
            )

        def quantize_z(b, lo, source):
            cols = slice(lo, lo + source.shape[1])
            nc.vector.quantize_mx(z_codes[b][:, cols].bitcast(FP8X4), z_scales[:, b, cols], source.rearrange("p m t -> p (m t)"))

        ahead = [(j, c) for c in range(2) for j in range(3)] + [(3, 0), (3, 1)]
        for a in range(PASSES):
            for j, c in ahead:
                first_product(j, c, a)
        empty(nc.scalar, (0, 0), (1, 0), (0, 1))
        empty(nc.vector, (2, 0), (1, 1), (2, 1), (3, 0))
        for j in range(PACK, SLOTS):
            for c in range(2):
                for a in range(PASSES):
                    first_product(j, c, a)
        w2_first = keep.tile([P, N, PACK], BF16, name="w2_first", align_bytes=64)
        weave_w2(0, w2_first, nc.gpsimd)
        pick_dest(0, 1, 2)
        pick_transfer(0, 1)
        add_gain(nc.gpsimd, 0, 1)
        pick_origin(0)
        empty(nc.vector, (3, 1), (4, 0), (4, 1))
        pick_dest(3)
        empty(nc.scalar, (5, 0))
        pick_dest(4)
        pick_transfer(2, 3)
        add_gain(nc.gpsimd, 2, 3)
        pick_origin(1)
        empty(nc.vector, (5, 1), (6, 0), (6, 1))
        pick_dest(5, 6)
        pick_transfer(4, 5)
        add_gain(nc.gpsimd, 4)
        pick_origin(2, 3)
        empty(nc.vector, (7, 0), (7, 1))
        pick_dest(7)
        pick_transfer(6)

        w2_codes = last.tile([P, GROUPS, N], U32, name="w2_codes", offset=LAST_AT + 2 * ROW - ROW, align_bytes=64)
        w2_scales = keep.tile([P, GROUPS, N], U8, name="w2_scales", align_bytes=64)

        def quantize_w2(b, lo, source):
            cols = slice(lo, lo + source.shape[1])
            nc.vector.quantize_mx(w2_codes[:, b, cols].bitcast(FP8X4), w2_scales[:, b, cols], source[:].rearrange("p n t -> p (n t)"))

        quantize_w2(0, 0, w2_first)
        pick_transfer(7)
        w2_rest = ending.tile([P, N, PACK], BF16, name="w2_rest", offset=0, align_bytes=64)
        weave_w2(1, w2_rest, nc.scalar)
        for lo, hi in ((0, HALF), (HALF, EARLY), (EARLY, LINES)):
            pick_origin(4, 5, 6, 7, lo=lo, hi=hi)
        add_gain(nc.vector, 5, 6, 7)
        woven0 = last.tile([P, LINES, PACK], BF16, name="woven0", offset=LAST_AT + 3 * ROW, align_bytes=64)
        for lo in (0, HALF):
            weave_z(0, lo, woven0[:, lo : lo + HALF])
        quantize_z(0, 0, woven0[:, 0:HALF])
        quantize_w2(1, 0, w2_rest)
        quantize_z(0, HALF, woven0[:, HALF:LINES])

        def second_product(target, n, b, cols, start, stop):
            nc.tensor.matmul_mx(
                target,
                lhsT=w2_codes[:, b, P * n : P * (n + 1)].bitcast(FP8X4),
                lhsT_scale=w2_scales[:, b, P * n : P * (n + 1)],
                rhs=z_codes[b][:, cols].bitcast(FP8X4),
                rhs_scale=z_scales[:, b, cols],
                start=start,
                stop=stop,
            )

        out_by_class = out.rearrange("(n p) m -> p n m", p=P)
        sums = [psum.tile([P, BANK], F32, name="bank", tag="bank") for cols in runs[:-1]]
        last_sums = [psum.tile([P, BANK], F32, name="bank", tag="bank") for n in range(classes)]
        for u, cols in enumerate(runs[:-1]):
            for n in range(classes):
                second_product(sums[u][:, P * n : P * (n + 1)], n, 0, cols, n == 0, False)
        for n in range(classes):
            second_product(last_sums[n][:, 0:P], n, 0, runs[-1], True, False)
        woven = [keep.tile([P, P, PACK], BF16, name=f"woven1{u}", align_bytes=64) for u in range(len(runs))]
        for u in range(len(runs)):
            weave_z(1, P * u, woven[u][:])
            if u:
                quantize_z(1, P * (u - 1), woven[u - 1][:])
        quantize_z(1, EARLY, woven[-1][:])
        for u, cols in enumerate(runs):
            result = keep.tile([P, classes, P], F32, name=f"result{u}")
            if u + 1 < len(runs):
                for n in range(classes):
                    second_product(sums[u][:, P * n : P * (n + 1)], n, 1, cols, False, n == classes - 1)
                nc.scalar.copy(result[:].rearrange("p n m -> p (n m)"), sums[u][:, 0 : classes * P])
            else:
                for n in range(classes):
                    second_product(last_sums[n][:, 0:P], n, 1, cols, False, True)
                    if n < 2:
                        nc.vector.tensor_copy(result[:, n, :], last_sums[n][:, 0:P])
                    else:
                        nc.scalar.copy(result[:, n, :], last_sums[n][:, 0:P])
            nc.sync.dma_start(out_by_class[:, :, cols], result[:])
